import numpy as np, ml_dtypes
CORES = [6,15,38,47]
N = 4
BF = ml_dtypes.bfloat16
def gentries(a):
    return np.ascontiguousarray(a.reshape(8, 16, -1).transpose(0, 2, 1)).reshape(8, -1)
def gtable(e):
    e = np.asarray(e); return np.ascontiguousarray(e.reshape(8, -1, 16).transpose(0, 2, 1)).reshape(128, -1).astype(np.int32)
ND, NR, L, CAP, HB, LV, RO = 2048, 4096, 256, 64, 2, 4, 3
def parts(rng):
    cold = rng.random((N, 8, 1, NR)) < 0.4; cold[..., 5] = True
    regs = rng.integers(-15, 16, (N, 8, 16, NR)); warm = rng.random(regs.shape) < rng.random((N, 8, 1, NR))
    regs = np.where(cold | ~warm, -np.abs(regs), regs)
    acts = rng.integers(0, NR, (N, 8, 16, ND)); dead = rng.random((N, 8, 1, ND)) < 0.125
    order = np.argsort(~cold[:, :, 0], axis=-1, kind="stable"); cnt = np.add.reduce(cold[:, :, 0].astype(np.int64), axis=-1)
    pick = (rng.random(acts.shape) * cnt[:, :, None, None]).astype(np.int64).reshape(N, 8, -1)
    acts = np.where(dead, np.take_along_axis(order, pick, 2).reshape(acts.shape), acts)
    return acts, regs, rng.integers(0, 16, (N, 8, 16, ND)), rng.integers(0, ND, (N, 8, L)), rng.integers(1, 16, (N, 8, 16, L)), rng.integers(0, 64, (N, 8, RO, LV, L))
def pack(acts, regs, pay, n0, rch, dr):
    b = lambda a: np.ascontiguousarray(a.reshape(N, 128, -1)).astype(np.float32).astype(BF)
    return {"acts": np.ascontiguousarray(acts.reshape(N, 128, ND)).astype(np.int32), "regs": b(regs), "pay": b(pay), "n0": np.stack([gtable(a) for a in n0]), "rch": b(rch),
            "dr": np.ascontiguousarray(dr.reshape(N, 8, RO * LV * L)).astype(np.int32)}
def setup_inputs(rng):
    return pack(*parts(rng))
def setup_inputs_room(rng):
    acts, regs, pay, n0, rch, dr = parts(rng)
    regs[:, ::2] = -rng.integers(2 * RO, 16, (N, 4, 16, NR)); pay = pay * rng.integers(0, 2, pay.shape)
    for q in range(N):
        for g in range(0, 8, 2):
            for t in range(RO):
                p = int(rng.integers(0, 4))
                if q == 0: p = (g // 2 + (t if g else 0)) % 4
                c = np.zeros(N, np.int64)
                if p == 0: c[:] = CAP
                elif p == 1: c[::2] = CAP + 1; c[1::2] = CAP - 1
                elif p == 2: c[0] = L
                else: c[1] = 1; c[2] = CAP; c[3] = L - 1 - CAP
                to = rng.permutation(np.repeat(np.arange(N), np.roll(c, int(rng.integers(0, N)))))
                dr[q, g, t, HB - 1] = to + N * rng.integers(0, 64 // N, L)
    return pack(acts, regs, pay, n0, rch, dr)
def setup_inputs_ties(rng):
    acts, regs, pay, n0, rch, dr = parts(rng)
    for g in (0, 3, 6):
        regs[:, g] = 15; rch[:, g] = rng.integers(1, 16 - 2 * RO, (N, 16, L))
        dr[:, g] = rng.choice(np.concatenate([4 * np.arange(16), 4 * np.arange(1, 16) - 1, np.array([63])]), (N, RO, LV, L))
    for g in (1, 4):
        i = rng.integers(0, 16, (N, 1, NR)); one = (np.arange(16)[None, :, None] == i) & (rng.random((N, 1, NR)) < 0.25)
        regs[:, g] = np.where(one, 1, -rng.integers(0, 16, (N, 16, NR)))
        dr[:, g] = 8 * rng.integers(0, 8, (N, RO, LV, L))
    for g in (2, 5, 7):
        dr[:, g] = rng.choice(np.array([0, 1, 31, 32, 62, 63]), (N, RO, LV, L))
    return pack(acts, regs, pay, n0, rch, dr)
def setup_inputs_alike(rng):
    acts, regs, pay, n0, rch, dr = parts(rng)
    n0[:, ::2] = rng.choice(np.array([0, ND - 1, ND // 2, 3]), (N, 4, L))
    acts[:, 1] = rng.choice(np.array([0, NR - 1, 7, NR // 2]), (N, 16, ND))
    acts[:, 5] = rng.integers(NR - 64, NR, (N, 16, ND)); acts[:, 7] = rng.integers(0, 100, (N, 16, ND))
    acts[:, 2] = acts[:, 2, :1]
    dr[:, 4:] = dr[:, 4:, :, :, :1]
    return pack(acts, regs, pay, n0, rch, dr)
def setup_inputs_clip(rng):
    acts, regs, pay, n0, rch, dr = parts(rng)
    regs = rng.choice(np.array([-15, -14, -1, 0, 1, 14, 15]), (N, 8, 16, NR)); pay = 15 * rng.integers(0, 2, pay.shape)
    rch = np.where(rng.random(rch.shape) < 0.7, 15, rng.integers(1, 3, rch.shape))
    a, b = rng.permutation(8)[:2]
    regs[:, a] = 15; rch[:, a] = 15; regs[:, b] = -15
    return pack(acts, regs, pay, n0, rch, dr)
def setup_inputs_spread(rng):
    acts, regs, pay, n0, rch, dr = parts(rng)
    u = lambda shape: np.minimum((np.exp2(4 * rng.random((N, 8, 1, shape[-1]))) * rng.random(shape)).astype(np.int64), 15)
    regs = u(regs.shape) * np.where(rng.random(regs.shape) < rng.random((N, 8, 1, NR)), 1, -1)
    pay = u(pay.shape); rch = np.maximum(u(rch.shape), 1)
    dr = np.minimum((64 * rng.random(dr.shape) ** np.exp2(4 * rng.random((N, 8, 1, 1, L)) - 2)).astype(np.int64), 63)
    return pack(acts, regs, pay, n0, rch, dr)
def check_inputs(d):
    bad = []
    for k, lo, hi in (("acts", 0, NR - 1), ("regs", -15, 15), ("pay", 0, 15), ("n0", 0, ND - 1), ("rch", 1, 15), ("dr", 0, 63)):
        a = np.asarray(d[k]).astype(np.float64)
        if not (np.min(a) >= lo and np.max(a) <= hi): bad.append("range of " + k)
        elif not np.all(a == np.rint(a)): bad.append("whole numbers in " + k)
    return bad
def level(rg, ac, n, x, v, e):
    S = n.shape[1]
    a = np.take_along_axis(ac, n[:, None, :], 2)
    p = np.maximum(np.take_along_axis(rg, a.reshape(8, 1, 16 * S), 2), 0).reshape(8, 16, 16, S)
    c = np.add.accumulate(np.add.reduce(np.minimum(x[:, :, None, :], p), axis=1), axis=1)
    tot = c[:, 15]
    k = np.where(tot > 0, np.argmax(64 * c > (v * tot)[:, None, :], axis=1), v & 15)
    rec = np.take_along_axis(a, k[:, None, :], 1)[:, 0]
    x = np.minimum(x, np.take_along_axis(p, k[:, None, None, :], 2)[:, :, 0] + 1)
    return k, rec, x, (5 * rec + 13 * n + e) & (ND - 1)
def rewrite(rg, rec, live, w):
    for g in range(8):
        s = np.nonzero(live[g])[0]
        u, j = np.unique(rec[g, s], return_index=True)
        rg[g][:, u] = np.clip(rg[g][:, u] + w[g][:, s[j]], -15, 15)
def reference(acts, regs, pay, n0, rch, dr):
    ac = acts.astype(np.int64).reshape(N, 8, 16, ND); rg = regs.astype(np.float32).astype(np.int64).reshape(N, 8, 16, NR)
    py = pay.astype(np.float32).astype(np.int64).reshape(N, 8, 16, ND); x0 = rch.astype(np.float32).astype(np.int64).reshape(N, 8, 16, L)
    st = np.stack([gentries(a) for a in n0]).astype(np.int64); v = dr.astype(np.int64).reshape(N, 8, RO, LV, L)
    for t in range(RO):
        fn = np.zeros((N, 8, N * CAP), np.int64); fx = np.ones((N, 8, 16, N * CAP), np.int64); fv = np.zeros((N, 8, LV, N * CAP), np.int64); live = np.zeros((N, 8, N * CAP), bool)
        home = []
        for r in range(N):
            n, x, vt = st[r], x0[r], v[r, :, t]
            for e in range(1, HB + 1): k, rec, x, n = level(rg[r], ac[r], n, x, vt[:, e - 1], e)
            to = k & (N - 1); oh = (to[:, None, :] == np.arange(N)[None, :, None]).astype(np.int64)
            place = np.take_along_axis(np.add.accumulate(oh, axis=2), to[:, None, :], 1)[:, 0] - 1
            g, l = np.nonzero(place < CAP); d = to[g, l]; s = r * CAP + place[g, l]
            fn[d, g, s] = n[g, l]; fx[d, g, :, s] = x[g, :, l]; fv[d, g, :, s] = vt[g, :, l]; live[d, g, s] = True
            home.append((rec, g, l, d, s))
        recs, sg = [], []
        for q in range(N):
            n, x = fn[q], fx[q]
            for e in range(HB + 1, LV + 1): k, rec, x, n = level(rg[q], ac[q], n, x, fv[q, :, e - 1], e)
            val = np.minimum(np.take_along_axis(py[q], n[:, None, :], 2), x)
            recs.append(rec); sg.append(np.sign(16 * val - np.add.reduce(val, axis=1, keepdims=True)))
        for q in range(N): rewrite(rg[q], recs[q], live[q], sg[q])
        sg = np.stack(sg)
        for r in range(N):
            rec, g, l, d, s = home[r]
            w = np.zeros((8, 16, L), np.int64); went = np.zeros((8, L), bool)
            w[g, :, l] = -sg[d, g, :, s]; went[g, l] = True
            rewrite(rg[r], rec, went, w)
    return {"yr": rg.reshape(N, 128, NR).astype(np.float32).astype(BF)}

@@ -1,0 +1,596 @@
+from concourse.bass import DstId, RemoteDMATransfer
+from concourse.mybir import dt, AluOpType, AxisListType, ActivationFunctionType
+
+N = 4
+RO = 3
+REG = 320
+EPS = 2.0 ** -30
+BETA = 2.0 ** -12
+HU = (128, 128)
+FU = ((0, 1), (2, 3))
+CG, CW, CS = 32, 64, 64
+
+F, B, H, I, U = "float32", "bfloat16", "float16", "int32", "uint16"
+
+
+def _scratch():
+    s, at = {}, {}
+    def sb(name, cols, d):
+        if cols > 1000 or name in ("rch_s", "n0_i", "dr_i") or name[:4] == "land":
+            s[name] = ("sbuf", [128, cols], d)
+        else:
+            big = "p" + d
+            lo = s[big][1][1] if big in s else 0
+            s[big] = ("sbuf", [128, lo + cols + -cols % 32], d)
+            at[name] = (big, lo, cols)
+    sb("acts_i", 2048, I); sb("regs_s", 4112, B); sb("P", 4096, B); sb("pay_s", 2048, B)
+    sb("rch_s", 256, B); sb("n0_i", 16, I); sb("dr_i", 256, I); sb("w_i", 256, I)
+    sb("drb", 256, B); sb("wb", 256, B)
+    sb("xr1", 4096, B); sb("xr", 4096, B); sb("W", 4096, B)
+    for e in (1, 2, 3, 4):
+        sb("A%d" % e, 256, U); sb("Ah%d" % e, 256, H); sb("q%d" % e, 256, H); sb("rec%d" % e, 16, U); sb("pre%d" % e, 16, F)
+    for e in (1, 2, 3, 4, 5):
+        sb("nU%d" % e, 16, U)
+    for n in ("y1", "y2", "y3", "yF3", "yF4", "yF5", "x5", "lv", "zF", "NV", "zl", "HV", "ms", "ind", "auxB", "auxF", "ng"):
+        sb(n, 256, B)
+    sb("t1", 256, F); sb("s_i", 16, I); sb("n_i", 16, I); sb("nlh", 32, I); sb("nlf", 32, F); sb("nx", 512, B)
+    for t in range(RO):
+        sb("vb%d" % t, 512, F); sb("wt%d" % t, 512, B); sb("auxS%d" % t, 256, B); sb("land%d" % t, 512, B); sb("zr%d" % t, 1280, B)
+    sb("vbF", 512, F); sb("wtF", 512, B)
+    sb("cum", 256, F); sb("Q", 256, H); sb("slot", 16, U); sb("send", 1280, B)
+    for n in ("h", "f"):
+        sb("rf8" + n, 16, F); sb("Y" + n, 256, F); sb("eq" + n, 256, B); sb("lc" + n, 256, B); sb("u" + n, 16, F); sb("off" + n, 32, U)
+    for u in range(4):
+        sb("mk%d" % u, 128, H); sb("mq%d" % u, 128, H)
+    sb("Dm", 128, I); sb("Bm", 128, I); sb("D12", 128, I); sb("pi", 2, I); sb("pk", 2, I); sb("rp", 256, I); sb("li", 256, I)
+    sb("crep", 256, U); sb("kf", 1, F); sb("pg", 1, F)
+    sb("BO", 128, B); sb("BO16", 128, H); sb("BO5", 128, H); sb("BOn", 128, B)
+    sb("ID", 128, B); sb("E1", 128, B); sb("E2", 128, B); sb("OHM", 128, B); sb("DST", 128, B)
+    sb("TRI", 128, B); sb("Z", 144, B); sb("ZM", 128, B)
+    sb("cols", 16, F); sb("SR", 640, B); sb("SEL", 768, B); sb("ZT", 864, B)
+    sb("rd", 256, F); sb("ta", 256, F); sb("tb", 256, F); sb("CMh", 256, B); sb("CMf", 256, B); sb("MX", 256, B)
+    sb("RST", 256, B); sb("ONE", 256, B); sb("SIX", 256, B)
+    for b in range(8):
+        s["b%d" % b] = ("psum", [128, 512], F)
+    return s, at
+
+
+SCRATCH, AT = _scratch()
+SEMAPHORES = (["eV", "eP", "eS", "eG"] + ["ld%d" % i for i in range(8)] + ["yo"]
+              + ["%s%d_%d" % (k, t, r) for k in ("a", "z", "la", "lz") for t in range(RO) for r in range(N)])
+
+
+def rank_program(g, core, T, topo):
+    me = T.rank_of(core)
+    if me is None:
+        return
+    OP, ACT = AluOpType, ActivationFunctionType
+    queue = {"V": g.vector, "P": g.tensor, "S": g.scalar, "G": g, "Y": g.sync}
+    count = {"eV": 0, "eP": 0, "eS": 0, "eG": 0}
+    known = {e: {} for e in queue}
+    free = {e: 0.0 for e in queue}
+    snap, acc, when = {}, {}, {}
+    CY, WAKE, GA, SC = 0.83, 100.0, 1.5, 3.0
+
+    def a(name, lo=None, hi=None, step=1, rows=128):
+        name, base, cols = AT.get(name, (name, 0, 0))
+        t = T[name]
+        if lo is None:
+            lo, hi = 0, cols or SCRATCH[name][1][1]
+        lo, hi = base + lo, base + hi
+        ap = t[0:rows, lo:hi] if step == 1 else t[0:rows, lo:hi:step]
+        return ap, [(name, lo, hi)], (hi - lo + step - 1) // step, 0
+
+    def via(win, off):
+        return win[0].indirect(off[0]), win[1] + off[1], 16 * off[2], 1
+
+    def narrow(x):
+        return SCRATCH[x[1][0][0]][2] in (B, U, H)
+
+    def merge(eng, tok):
+        k = known[eng]
+        for s, v in list(snap.get(tok, {}).items()) + [tok]:
+            if k.get(s, 0) < v:
+                k[s] = v
+
+    def needs(eng, reads, writes):
+        need = {}
+        for regs, w in ((reads, False), (writes, True)):
+            for name, lo, hi in regs:
+                bank = SCRATCH[name][0] == "psum"
+                for (e2, tok, l2, h2, w2) in acc.get(name, []):
+                    if bank and e2 != eng:
+                        hit = True
+                    elif l2 < hi and lo < h2:
+                        if w and w2:
+                            hit = not (eng == "P" and e2 == "P")
+                        elif w:
+                            hit = e2 != eng
+                        else:
+                            hit = w2
+                    else:
+                        hit = False
+                    if hit and known[eng].get(tok[0], 0) < tok[1] and need.get(tok[0], 0) < tok[1]:
+                        need[tok[0]] = tok[1]
+        return need
+
+    def order(eng, reads, writes):
+        need = needs(eng, reads, writes)
+        for s in sorted(need):
+            v = need[s]
+            if any(s2 != s and snap.get((s2, need[s2]), {}).get(s, 0) >= v for s2 in need):
+                need[s] = 0
+        for s in sorted(need):
+            if need[s]:
+                queue[eng].wait_ge(T.sem[s], need[s])
+                merge(eng, (s, need[s]))
+
+    def record(eng, tok, reads, writes):
+        for regs, w in ((reads, False), (writes, True)):
+            for name, lo, hi in regs:
+                old = acc.get(name, [])
+                keep = [x for x in old if not (lo <= x[2] and x[3] <= hi and (w or (x[0] == eng and not x[4])))]
+                keep.append((eng, tok, lo, hi, w))
+                acc[name] = keep
+
+    def start(op):
+        eng, call, reads, writes, dur = op[:5]
+        t = free[eng]
+        for s, v in needs(eng, reads, writes).items():
+            t = max(t, when.get((s, v), 0.0) + WAKE)
+        return t
+
+    def done(tok, eng, t):
+        sn = dict(known[eng]); sn[tok[0]] = tok[1]
+        snap[tok] = sn
+        when[tok] = t
+
+    def do(op):
+        eng, call, reads, writes, dur = op[:5]
+        t = start(op)
+        order(eng, reads, writes)
+        free[eng] = t + dur
+        if len(op) > 5:
+            call()
+            done(op[5], eng, t + 3000.0)
+            record("R" + op[5][0], op[5], reads, [])
+            return
+        s = "e" + eng
+        count[s] += 1
+        call().then_inc(T.sem[s], 1)
+        done((s, count[s]), eng, t + dur)
+        record(eng, (s, count[s]), reads, writes)
+
+    def together(jobs):
+        jobs = [[p, j, None] for p, j in jobs]
+        live = list(jobs)
+        while live:
+            best = None
+            for x in list(live):
+                while not isinstance(x[2], tuple) and x[2] != "end":
+                    if x[2] is None:
+                        x[2] = next(x[1], "end")
+                    elif x[2]():
+                        x[2] = None
+                    else:
+                        break
+                if x[2] == "end":
+                    live.remove(x)
+                elif isinstance(x[2], tuple):
+                    k = (start(x[2]), x[0])
+                    if best is None or k < best[0]:
+                        best = (k, x)
+            if best:
+                do(best[1][2])
+                best[1][2] = None
+
+    def regs_of(*xs):
+        return [r for x in xs if isinstance(x, tuple) for r in x[1]]
+
+    def val(x):
+        return x[0] if isinstance(x, tuple) else x
+
+    def vop(call, out, ins, n, wide=1.0):
+        x = [i for i in ins if i[3]]
+        d = x[0][2] * GA * CY if x else out[2] * SC * CY if out[3] else max(64.0, n * wide) * CY
+        return ("V", call, regs_of(*ins), out[1], 60.0 + d)
+
+    def ts(out, in0, s1, op0, s2=None, op1=None):
+        if op1 is None:
+            f = lambda: g.vector.tensor_scalar(out[0], in0[0], val(s1), None, op0)
+        else:
+            f = lambda: g.vector.tensor_scalar(out[0], in0[0], val(s1), val(s2), op0, op1)
+        return vop(f, out, [in0] + [x for x in (s1, s2) if isinstance(x, tuple)], in0[2], 0.5 if narrow(out) and narrow(in0) else 1.0)
+
+    def tt(out, in0, in1, op):
+        ps = any(SCRATCH[x[1][0][0]][0] == "psum" for x in (in0, in1))
+        return vop(lambda: g.vector.tensor_tensor(out[0], in0[0], in1[0], op), out, [in0, in1], in1[2], 1.0 if ps else 2.0)
+
+    def cp(out, in_):
+        return vop(lambda: g.vector.tensor_copy(out[0], in_[0]), out, [in_], in_[2])
+
+    def scatter(win, off, in_):
+        return vop(lambda: g.vector.tensor_copy(win[0].indirect(off[0]), in_[0]), (None, win[1], in_[2], 1), [in_, off], in_[2])
+
+    def fill(out, c):
+        return vop(lambda: g.vector.memset(out[0], c), out, [], out[2], 0.5)
+
+    def scan(out, d0, d1, init):
+        return vop(lambda: g.vector.tensor_tensor_scan(out[0], d0[0], d1[0], val(init), OP.mult, OP.add), out,
+                   [d0, d1] + [x for x in (init,) if isinstance(x, tuple)], d1[2], 0.5 if narrow(out) and narrow(d1) else 1.0)
+
+    def act(out, in_, func, bias=0.0, scale=1.0):
+        if func == ACT.Copy:
+            f = lambda: g.scalar.activation(out[0], in_[0], func, scale=scale)
+        else:
+            f = lambda: g.scalar.activation(out[0], in_[0], func, bias=val(bias), scale=scale)
+        return ("S", f, regs_of(in_, bias), out[1], 65.0 + in_[2] * GA * CY if in_[3] else 165.0 + in_[2] * CY)
+
+    def mm(out, lhsT, rhs, start=True, stop=True):
+        return ("P", lambda: g.tensor.matmul(out[0], lhsT[0], rhs[0], start, stop), regs_of(lhsT, rhs), out[1], 10.0 + max(64, rhs[2]) * CY)
+
+    def iota(out, pattern, base, ch):
+        return ("G", lambda: g.iota(out[0], pattern, base, ch), [], out[1], 130.0 + 2 * out[2] * CY)
+
+    def load(eng, sem, out, src, reg):
+        order(eng, [], reg)
+        queue[eng].dma_start(out, src).then_inc(T.sem[sem], 16)
+        done((sem, 16), eng, 3000.0 + 1500.0 * (SCRATCH[reg[0][0]][1][1] > 1000))
+        record("D" + sem, (sem, 16), [], reg)
+
+    def send(r, src, dst, sem, lsem):
+        rid, pid, _ = topo.addr(T.cores[r])
+        m = sum(1 << x for x in topo.engines(core, T.cores[r])[:8])
+        return ("G", lambda: g.remote_dma(dst, src[0], T.sem[sem], T.sem[lsem], pid, rid, m), regs_of(src), [], 300.0, (lsem, 8))
+
+    def arrives(sem, regions, t):
+        snap[(sem, 8)] = {sem: 8}
+        when[(sem, 8)] = t
+        record("R" + sem, (sem, 8), [], regions)
+
+    def far_key(r):
+        c1, c2 = topo.chip(core), topo.chip(T.cores[r])
+        return 0 if topo.mates(c1, c2) else 1 if topo.same_plane(c1, c2) else 2
+    others = sorted([r for r in range(N) if r != me], key=far_key)
+    place = [me] + others
+    def units(sizes):
+        out, lo = [], 0
+        for n in sizes:
+            out.append((lo, lo + n))
+            lo += n
+        return out
+    HUN = units(HU)
+    FUN = units([64 * len(p) for p in FU])
+
+    load("Y", "ld0", T.n0_i[:], T.n0[:], [("n0_i", 0, 16)])
+    load("S", "ld1", T.rch_s[:], T.rch[:], [("rch_s", 0, 256)])
+    load("Y", "ld2", T.acts_i[:], T.acts[:], [("acts_i", 0, 2048)])
+    load("S", "ld3", T.dr_i[0:96, :], T.dr[:, :], [("dr_i", 0, 256)])
+    load("S", "ld4", T.regs_s[:, 0:2048], T.regs[:, 0:2048], [("regs_s", 0, 2048)])
+    load("Y", "ld5", T.regs_s[:, 2048:4096], T.regs[:, 2048:4096], [("regs_s", 2048, 4096)])
+    load("Y", "ld6", T.pay_s[:], T.pay[:], [("pay_s", 0, 2048)])
+
+    kf = a("kf")
+    def col(j):
+        return a("cols", j, j + 1)
+    home_te = [4 * t + e for t in range(RO) for e in (0, 1)]
+    far_te = [4 * t + e for t in range(RO) for e in (2, 3)]
+    marks = {}
+
+    def mark(k):
+        return lambda: k in marks
+
+    def constants():
+        yield iota(a("li"), [[1, 256]], 0, 0)
+        yield iota(a("pi"), [[0, 2]], 0, 1)
+        yield iota(a("Bm"), [[1, 8], [0, 16]], 0, 0)
+        yield iota(a("Dm"), [[1, 128]], 0, -1)
+        yield iota(a("D12"), [[-12, 8], [0, 16]], 0, 1)
+        yield iota(a("rp"), [[0, 16], [1, 16]], 0, 0)
+        yield cp(a("crep"), a("li"))
+        yield cp(a("nU1"), a("n0_i"))
+        yield ts(a("pk", 0, 1), a("pi", 0, 1), 15, OP.bitwise_and)
+        yield ts(a("pk", 1, 2), a("pi", 1, 2), 4, OP.arith_shift_right)
+        yield cp(a("kf"), a("pk", 0, 1))
+        yield cp(a("pg"), a("pk", 1, 2))
+        yield fill(col(3), BETA)
+        yield fill(col(14), 1.0)
+        yield ts(a("BO"), a("Bm"), a("pg"), OP.is_equal)
+        yield fill(a("Z"), 0.0)
+        yield cp(a("Z", 15, 143, 16), a("BO", 0, 128, 16))
+        for u in range(4):
+            yield act(a("xr1", 1024 * u, 1024 * u + 1024), via(a("rch_s", 64 * u, 64 * u + 64), a("crep", 0, 64)), ACT.Copy)
+        yield ts(a("BO16"), a("BO"), 1.0, OP.mult)
+        yield ts(a("BO5"), a("BO"), 5.0, OP.mult)
+        yield ts(a("rd"), a("rp"), kf, OP.subtract)
+        yield ts(a("MX"), a("rd"), 0.0, OP.is_equal)
+        yield ts(a("ID"), a("Dm"), 0, OP.is_equal)
+        yield ts(a("TRI"), a("Dm"), 0, OP.is_ge, 64.0, OP.mult)
+        yield tt(a("TRI"), a("TRI"), a("BO"), OP.mult)
+        yield fill(a("TRI", 15, 128, 16), 0.0)
+        yield ts(col(0), kf, 15.0, OP.is_lt)
+        yield ts(a("E1"), a("Dm"), 1, OP.is_equal)
+        yield ts(a("E2"), a("Dm"), -15, OP.is_equal)
+        yield tt(a("E1"), a("E1"), a("E2"), OP.add)
+        yield tt(a("E1"), a("E1"), a("BO"), OP.mult)
+        yield ts(a("E2"), a("ID"), col(0), OP.mult)
+        yield tt(a("OHM"), a("E1"), a("E2"), OP.subtract)
+        yield ts(col(1), kf, -EPS, OP.mult)
+        yield ts(col(2), kf, 15.0, OP.is_equal, 16 * EPS, OP.mult)
+        yield tt(col(1), col(1), col(2), OP.add)
+        yield cp(a("drb", rows=96), a("dr_i", rows=96))
+        yield ts(a("w_i", rows=96), a("dr_i", rows=96), 15, OP.bitwise_and)
+        yield cp(a("wb", rows=96), a("w_i", rows=96))
+        for j in range(6):
+            yield ts(a("SEL", 128 * j, 128 * j + 128, rows=96), a("D12", rows=96), home_te[j], OP.is_equal)
+        yield ts(a("y1"), a("rch_s"), -1.0, OP.add)
+        yield ts(a("pre1"), a("n0_i"), 13.0, OP.mult, 1.0 + 10240.0, OP.add)
+        for x in draws(0):
+            yield x
+        for n, c in ([("DST", 0.0), ("ZT", 0.0), ("ONE", 1.0), ("SIX", 0.0625), ("send", 0.0)]):
+            yield fill(a(n), c)
+        for d in range(4):
+            yield tt(a("DST", d, 128, 16), a("OHM", d, 128, 16), a("OHM", d + 4, 128, 16), OP.add)
+            yield tt(a("DST", d, 128, 16), a("DST", d, 128, 16), a("OHM", d + 8, 128, 16), OP.add)
+            yield tt(a("DST", d, 128, 16), a("DST", d, 128, 16), a("OHM", d + 12, 128, 16), OP.add)
+        yield ts(col(4), kf, 320.0, OP.mult, -1.0, OP.add)
+        yield ts(col(5), kf, 320.0, OP.mult, 64.0, OP.add)
+        yield ts(col(6), kf, 4096.0, OP.add)
+        for j in range(6):
+            yield ts(a("ZT", 144 * j + 15, 144 * j + 143, 16, rows=96), a("D12", 0, 128, 16, rows=96), far_te[j], OP.is_equal)
+        for x in aux_static(0):
+            yield x
+        marks["c"] = 1
+        yield ts(col(7), kf, 2.0, OP.is_equal)
+        yield ts(col(8), kf, 3.0, OP.is_equal, 256.0, OP.mult)
+        yield tt(col(7), col(7), col(8), OP.add)
+        yield ts(a("BOn"), a("BO"), col(7), OP.mult)
+        for j, (row, w) in enumerate(((0, 1.0), (1, 1.0), (5, 1.0), (6, 1.0), (4, -8192.0))):
+            yield ts(col(9 + j), kf, float(row), OP.is_equal, w, OP.mult)
+            yield ts(a("SR", 128 * j, 128 * j + 128), a("BO"), col(9 + j), OP.mult)
+        for t in range(RO):
+            yield fill(a("zr%d" % t), 0.0)
+        yield ts(a("ZM"), a("ID"), 16.0, OP.mult)
+        yield tt(a("ZM"), a("ZM"), a("BO"), OP.subtract)
+        yield ts(a("ta"), a("rd"), 0.0, OP.is_gt, 16384.0, OP.mult)
+        yield ts(a("tb"), a("rd"), 0.0, OP.is_equal, -8192.0, OP.mult)
+        yield tt(a("ta"), a("ta"), a("tb"), OP.add)
+        yield ts(a("CMh"), a("ta"), 2048.0, OP.add)
+        yield ts(a("CMf"), a("ta"), 10240.0, OP.add)
+        yield ts(a("RST"), a("rp"), 0, OP.is_gt)
+        marks["e"] = 1
+
+    def draws(t):
+        for src, b in (("drb", "b6"), ("wb", "b7")):
+            for j in (0, 1):
+                s = 128 * (2 * t + j)
+                yield mm(a(b, 256 * j, 256 * j + 256), a("SEL", s, s + 128, rows=96), a(src, rows=96))
+            if src == "drb":
+                yield act(a("vb%d" % t), a(b), ACT.Identity, bias=col(3))
+            else:
+                yield act(a("wt%d" % t), a(b), ACT.Relu, bias=col(1), scale=EPS)
+        marks["v%d" % t] = 1
+
+    def aux_static(t):
+        for k, (src, j, row) in enumerate((("drb", 0, 0), ("drb", 1, 1), ("wb", 0, 5), ("wb", 1, 6))):
+            s = 144 * (2 * t + j) + 15 - row
+            yield mm(a("b7", 0, 256), a("ZT", s, s + 128, rows=96), a(src, rows=96), k == 0, False)
+        yield mm(a("b7", 0, 256), a("Z", 11, 139), a("SIX"), False, True)
+        yield act(a("auxS%d" % t), a("b7", 0, 256), ACT.Copy)
+        marks["x%d" % t] = 1
+
+    def relu_records():
+        yield ts(a("P", 0, 2736), a("regs_s", 0, 2736), 0.0, OP.max)
+        yield act(a("P", 2736, 4096), a("regs_s", 2736, 4096), ACT.Relu)
+        marks["P"] = 1
+
+    def acts_at(e, lo, hi):
+        return cp(a("A%d" % e, lo, hi), via(a("acts_i"), a("nU%d" % e, lo // 16, hi // 16)))
+
+    def acts_half(e, lo, hi):
+        return ts(a("Ah%d" % e, lo, hi), a("A%d" % e, lo, hi), -2048.0, OP.add)
+
+    YN = {1: "y1", 2: "y2", 3: "yF3", 4: "yF4"}
+    YO = {1: "y2", 2: "y3", 3: "yF4", 4: "yF5"}
+
+    def spread(e, lo, hi):
+        for l in range(lo, hi, CS):
+            n = min(CS, hi - l)
+            yield act(a("xr", 16 * l, 16 * l + 16 * n), via(a(YN[e], l, l + n), a("crep", 0, n)), ACT.Identity, bias=col(14))
+
+    def diag(b1, c1, src, ones, mk, b2, c2, last, n, lo, hi):
+        yield mm(a(b1, c1, c1 + 128, rows=n), a(src, lo, hi), a(ones))
+        yield tt(a(mk, rows=n), a(b1, c1, c1 + 128, rows=n), a("MX", 0, 128, rows=n), OP.mult)
+        yield mm(a(b2, c2, c2 + n // 16), a(mk, rows=n), a(last, 0, n, 16, rows=n))
+
+    def level(e, t, u, lo, hi):
+        n = hi - lo
+        bank = "b%d" % u
+        tl, th = lo // 16, hi // 16
+        x = "xr1" if e == 1 else "xr"
+        vb, wt = ("vb%d" % t, "wt%d" % t) if e < 3 else ("vbF", "wtF")
+        at = 256 * ((e - 1) % 2)
+        for l in range(lo, hi, CW):
+            m = min(CW, hi - l)
+            for j in range(l, l + m, CG):
+                c = min(CG, l + m - j)
+                yield tt(a("W", 16 * j, 16 * j + 16 * c), via(a("P"), a("A%d" % e, j, j + c)), a(x, 16 * j, 16 * j + 16 * c), OP.min)
+            if e == 1:
+                yield mark("v%d" % t)
+            for k in range(16):
+                yield mm(a(bank, l - lo, l - lo + m), a("Z", 15 - k, 143 - k), a("W", 16 * l + k, 16 * l + 16 * m, 16), k == 0, k == 15)
+        yield act(a("ms", lo, hi), a(bank, 0, n), ACT.Copy)
+        yield mm(a(bank, n, 2 * n), a("ID"), a(wt, at + lo, at + hi), True, False)
+        yield mm(a(bank, n, 2 * n), a("BO"), a("ms", lo, hi), False, True)
+        yield mm(a(bank, 2 * n, 3 * n), a("TRI"), a("ms", lo, hi))
+        yield tt(a("t1", lo, hi), a(bank, n, 2 * n), a(vb, at + lo, at + hi), OP.mult)
+        yield tt(a("ind", lo, hi), a(bank, 2 * n, 3 * n), a("t1", lo, hi), OP.is_lt)
+        yield mm(a(bank, 3 * n, 4 * n), a("OHM"), a("ind", lo, hi))
+        if e == 2:
+            yield mark("c")
+            yield mm(a("b4", lo, hi), a("DST"), a("ind", lo, hi))
+        yield tt(a("q%d" % e, lo, hi), a(bank, 3 * n, 4 * n), a("Ah%d" % e, lo, hi), OP.mult)
+        for o in diag(bank, 0, "q%d" % e, "BO16", "mk%d" % u, bank, n, "BO5", n, lo, hi):
+            yield o
+        if e == 2:
+            yield lambda: lo == 0 or "s%d_%d" % (t, lo) in marks
+            yield scan(a("cum", lo, hi), a("ONE", lo, hi), a("b4", lo, hi), col(4) if lo == 0 else a("cum", lo - 1, lo))
+            marks["s%d_%d" % (t, hi)] = 1
+            yield tt(a("Q", lo, hi), a("b4", lo, hi), a("cum", lo, hi), OP.mult)
+            for o in diag("b5", 128 * u, "Q", "BO16", "mq%d" % u, "b4", 256 + tl, "BO16", n, lo, hi):
+                yield o
+        p = a(bank, n, n + n // 16)
+        if e == 2:
+            yield tt(a("s_i", tl, th), p, a("pre%d" % e, tl, th), OP.add)
+        yield ts(a("rec%d" % e, tl, th), p, 0.2, OP.mult, 2048.25, OP.add)
+        yield tt(a(YO[e], lo, hi), via(a("P"), a("rec%d" % e, tl, th)), a(YN[e], lo, hi), OP.min)
+        if e in (1, 3):
+            for o in spread(e + 1, lo, hi):
+                yield o
+        if e != 2:
+            yield tt(a("s_i", tl, th), p, a("pre%d" % e, tl, th), OP.add)
+        yield ts(a("n_i", tl, th), a("s_i", tl, th), 2047, OP.bitwise_and)
+        if e != 2:
+            yield cp(a("nU%d" % (e + 1), tl, th), a("n_i", tl, th))
+        if e in (1, 3):
+            yield acts_at(e + 1, lo, hi)
+            yield ts(a("pre%d" % (e + 1), tl, th), a("n_i", tl, th), 13.0, OP.mult, e + 1.0 + 10240.0, OP.add)
+            yield acts_half(e + 1, lo, hi)
+
+    def home(t, u, lo, hi):
+        tl, th = lo // 16, hi // 16
+        if t == 0:
+            yield acts_at(1, lo, hi)
+            yield acts_half(1, lo, hi)
+        yield mark("P")
+        for e in (1, 2):
+            for o in level(e, t, u, lo, hi):
+                yield o
+        yield ts(a("nlh", tl, th), a("n_i", tl, th), 255, OP.bitwise_and)
+        yield ts(a("nlh", 16 + tl, 16 + th), a("n_i", tl, th), 8, OP.arith_shift_right)
+        yield cp(a("slot", tl, th), a("b4", 256 + tl, 256 + th))
+        yield cp(a("nlf", tl, th), a("nlh", tl, th))
+        yield cp(a("nlf", 16 + tl, 16 + th), a("nlh", 16 + tl, 16 + th))
+        yield tt(a("nx", lo, hi), via(a("nlf", 0, 16), a("crep", tl, th)), a("MX", lo, hi), OP.mult)
+        yield tt(a("nx", 256 + lo, 256 + hi), via(a("nlf", 16, 32), a("crep", tl, th)), a("MX", lo, hi), OP.mult)
+        yield mark("x%d" % t)
+        yield mm(a("b6", lo, hi), a("ID"), a("auxS%d" % t, lo, hi), True, False)
+        yield mm(a("b6", lo, hi), a("Z", 13, 141), a("nx", lo, hi), False, False)
+        yield mm(a("b6", lo, hi), a("Z", 12, 140), a("nx", 256 + lo, 256 + hi), False, True)
+        yield act(a("auxB", lo, hi), a("b6", lo, hi), ACT.Copy)
+        yield scatter(a("send", 0, 1216), a("slot", tl, th), a("y3", lo, hi))
+        marks["y%d_%d" % (t, lo)] = 1
+        yield lambda: all("y%d_%d" % (t, l) in marks for l, h in HUN)
+        yield scatter(a("send", 64, 1280), a("slot", tl, th), a("auxB", lo, hi))
+
+    def depart(t):
+        for r in others:
+            do(send(r, a("send", REG * r, REG * r + 128), T["land%d" % t][:, 128 * me:128 * me + 128], "a%d_%d" % (t, me), "la%d_%d" % (t, r)))
+        for i, r in enumerate(others):
+            arrives("a%d_%d" % (t, r), [("land%d" % t, 128 * r, 128 * r + 128)], free["G"] + 2700.0 + 500.0 * i)
+            arrives("z%d_%d" % (t, r), [("zr%d" % t, REG * r, REG * r + 64)], free["G"] + 30000.0)
+
+    def far(t, u, ps, lo, hi):
+        tl, th = lo // 16, hi // 16
+        n = hi - lo
+        bank = "b%d" % u
+        for p in ps:
+            name, s = ("send", REG * me) if p == 0 else ("land%d" % t, 128 * place[p])
+            yield act(a("auxF", 64 * p, 64 * p + 64), a(name, s + 64, s + 128), ACT.Copy)
+            yield act(a("yF3", 64 * p, 64 * p + 64), a(name, s, s + 64), ACT.Copy)
+        for o in spread(3, lo, hi):
+            yield o
+        for o in diag("b5", 128 * u, "auxF", "BOn", "mq%d" % u, "b4", tl, "BO16", n, lo, hi):
+            yield o
+        for j in (0, 2, 1, 3):
+            yield mm(a(bank, n * j, n * j + n), a("SR", 128 * j, 128 * j + 128), a("auxF", lo, hi))
+        yield cp(a("nU3", tl, th), a("b4", tl, th))
+        yield acts_at(3, lo, hi)
+        for j in (0, 1):
+            yield act(a("vbF", 256 * j + lo, 256 * j + hi), a(bank, n * j, n * j + n), ACT.Identity, bias=col(3))
+            yield act(a("wtF", 256 * j + lo, 256 * j + hi), a(bank, n * (2 + j), n * (3 + j)), ACT.Relu, bias=col(1), scale=EPS)
+        yield ts(a("pre3", tl, th), a("b4", tl, th), 13.0, OP.mult, 3.0 + 10240.0, OP.add)
+        yield acts_half(3, lo, hi)
+        for e in (3, 4):
+            for o in level(e, t, u, lo, hi):
+                yield o
+        yield act(a("x5", lo, hi), a("yF5", lo, hi), ACT.Identity, bias=col(14))
+        yield tt(a("lv", lo, hi), via(a("pay_s"), a("nU5", tl, th)), a("x5", lo, hi), OP.min)
+        yield mm(a(bank, 0, n), a("ZM"), a("lv", lo, hi))
+        yield act(a("zF", lo, hi), a(bank, 0, n), ACT.Sign)
+        for p in ps:
+            r = place[p]
+            if p:
+                yield send(r, a("zF", 64 * p, 64 * p + 64), T["zr%d" % t][:, REG * me:REG * me + 64], "z%d_%d" % (t, me), "lz%d_%d" % (t, r))
+            else:
+                yield act(a("zr%d" % t, REG * me, REG * me + 64), a("zF", 0, 64), ACT.Copy)
+        yield tt(a("NV", lo, hi), via(a("regs_s", 0, 4096), a("rec4", tl, th)), a("zF", lo, hi), OP.add)
+        yield ts(a("NV", lo, hi), a("NV", lo, hi), 15.0, OP.min, -15.0, OP.max)
+        marks["f%d_%d" % (t, u)] = 1
+
+    def first_of(n, q, cm, extra, rec):
+        yield ts(a("rf8" + n), a(rec), 2.0 ** -13, OP.mult)
+        yield mm(a("b7", 0, 256), a("BO16"), a(q), True, False)
+        yield mm(a("b7", 0, 256), a("ID"), a(cm), False, False)
+        yield mm(a("b7", 0, 256), extra[0], extra[1], False, True)
+        yield act(a("Y" + n), via(a("rf8" + n), a("crep", 0, 16)), ACT.Copy, scale=8192.0)
+        yield tt(a("eq" + n), a("b7", 0, 256), a("Y" + n), OP.is_equal)
+        yield scan(a("lc" + n), a("RST"), a("eq" + n), 0.0)
+        yield tt(a("u" + n), a("lc" + n, 15, 256, 16), a("rf8" + n), OP.add)
+        yield ts(a("off" + n, 0, 32, 2), a("u" + n), 8192.0, OP.mult, col(6), OP.min)
+
+    def change(n, blocks, values):
+        for c in blocks:
+            yield scatter(a("regs_s"), a("off" + n, 2 * c, 2 * c + 1), a(values, 16 * c, 16 * c + 16))
+
+    def waiting(t):
+        yield mark("e")
+        yield ts(a("ng"), a("Q"), col(5), OP.is_ge, 8192.0, OP.mult)
+        for o in first_of("h", "q2", "CMh", (a("BO"), a("ng")), "rec2"):
+            yield o
+        if t + 1 < RO:
+            for o in draws(t + 1):
+                yield o
+            for o in aux_static(t + 1):
+                yield o
+
+    def leaves(t):
+        yield lambda: all("f%d_%d" % (t, u) in marks for u in range(len(FUN)))
+        for o in first_of("f", "q4", "CMf", (a("SR", 512, 640), a("auxF")), "rec4"):
+            yield o
+        for o in change("f", [4 * place.index(r) + c for r in (3, 2, 1, 0) for c in (3, 2, 1, 0)], "NV"):
+            yield o
+        if t + 1 < RO:
+            yield fill(a("send"), 0.0)
+        for lo in range(0, 256, 64):
+            yield act(a("zl", lo, lo + 64), via(a("zr%d" % t), a("slot", lo // 16, lo // 16 + 4)), ACT.Copy, scale=-1.0)
+        yield tt(a("HV"), via(a("regs_s", 0, 4096), a("rec2")), a("zl"), OP.add)
+        yield ts(a("HV"), a("HV"), 15.0, OP.min, -15.0, OP.max)
+        for o in change("h", list(range(15, -1, -1)), "HV"):
+            yield o
+
+    for t in range(RO):
+        jobs = [(u, home(t, u, lo, hi)) for u, (lo, hi) in enumerate(HUN)]
+        if t == 0:
+            c = constants()
+            for i in range(17):
+                do(next(c))
+            together([(9, c), (8, relu_records())] + jobs)
+        else:
+            for o in relu_records():
+                do(o)
+            together(jobs)
+        depart(t)
+        together([(u, far(t, u, FU[u], lo, hi)) for u, (lo, hi) in enumerate(FUN)] + [(8, waiting(t)), (7, leaves(t))])
+
+    order("Y", [("regs_s", 0, 4112)], [])
+    g.sync.dma_start(T.yr[:], T.regs_s[:, 0:4096]).then_inc(T.sem.yo, 16)
+    g.sync.wait_ge(T.sem.yo, 16)
+    for s in ("eV", "eP", "eS", "eG"):
+        g.sync.wait_ge(T.sem[s], count[s])
+    for i in range(7):
+        g.sync.wait_ge(T.sem["ld%d" % i], 16)
+    for t in range(RO):
+        for r in others:
+            for k in ("a", "z", "la", "lz"):
+                g.sync.wait_ge(T.sem["%s%d_%d" % (k, t, r)], 8)

@@ -7,8 +7,8 @@ REG = 320
 EPS = 2.0 ** -30
 BETA = 2.0 ** -12
 HU = (128, 128)
-FU = ((0, 1), (2, 3))
-CG, CW, CS = 32, 64, 64
+FU = ((0,), (1, 2), (3,))
+CG, CW, CS = 64, 64, 64
 
 F, B, H, I, U = "float32", "bfloat16", "float16", "int32", "uint16"
 
@@ -16,14 +16,14 @@ F, B, H, I, U = "float32", "bfloat16", "float16", "int32", "uint16"
 def _scratch():
     s, at = {}, {}
     def sb(name, cols, d):
-        if cols > 1000 or name in ("rch_s", "n0_i", "dr_i") or name[:4] == "land":
+        if cols > 1024 or name in ("rch_s", "n0_i", "dr_i") or name[:4] == "land":
             s[name] = ("sbuf", [128, cols], d)
         else:
             big = "p" + d
             lo = s[big][1][1] if big in s else 0
             s[big] = ("sbuf", [128, lo + cols + -cols % 32], d)
             at[name] = (big, lo, cols)
-    sb("acts_i", 2048, I); sb("regs_s", 4112, B); sb("P", 4096, B); sb("pay_s", 2048, B)
+    sb("acts_i", 2048, I); sb("regs_s", 4128, B); sb("P", 4096, B); sb("pay_s", 2048, B); sb("paym", 2048, B)
     sb("rch_s", 256, B); sb("n0_i", 16, I); sb("dr_i", 256, I); sb("w_i", 256, I)
     sb("drb", 256, B); sb("wb", 256, B)
     sb("xr1", 4096, B); sb("xr", 4096, B); sb("W", 4096, B)
@@ -31,21 +31,22 @@ def _scratch():
         sb("A%d" % e, 256, U); sb("Ah%d" % e, 256, H); sb("q%d" % e, 256, H); sb("rec%d" % e, 16, U); sb("pre%d" % e, 16, F)
     for e in (1, 2, 3, 4, 5):
         sb("nU%d" % e, 16, U)
-    for n in ("y1", "y2", "y3", "yF3", "yF4", "yF5", "x5", "lv", "zF", "NV", "zl", "HV", "ms", "ind", "auxB", "auxF", "ng"):
+    for n in ("y1", "y2", "y3", "yF3", "yF4", "yF5", "lv", "zF", "NV", "zl", "HV", "ms", "ind", "auxB", "auxF", "ng"):
         sb(n, 256, B)
-    sb("t1", 256, F); sb("s_i", 16, I); sb("n_i", 16, I); sb("nlh", 32, I); sb("nlf", 32, F); sb("nx", 512, B)
+    sb("t1", 256, F); sb("s_i", 16, I); sb("n_i", 16, I); sb("nlf", 64, B); sb("nx", 1024, B)
     for t in range(RO):
         sb("vb%d" % t, 512, F); sb("wt%d" % t, 512, B); sb("auxS%d" % t, 256, B); sb("land%d" % t, 512, B); sb("zr%d" % t, 1280, B)
     sb("vbF", 512, F); sb("wtF", 512, B)
     sb("cum", 256, F); sb("Q", 256, H); sb("slot", 16, U); sb("send", 1280, B)
     for n in ("h", "f"):
-        sb("rf8" + n, 16, F); sb("Y" + n, 256, F); sb("eq" + n, 256, B); sb("lc" + n, 256, B); sb("u" + n, 16, F); sb("off" + n, 32, U)
+        sb("rf8" + n, 16, F); sb("Y" + n, 256, F); sb("eq" + n, 256, B); sb("lc" + n, 256, B); sb("u" + n, 16, F)
+        sb("off" + n, 16, U); sb("Z2" + n, 256, F); sb("er" + n, 256, B); sb("ld" + n, 256, B)
     for u in range(4):
         sb("mk%d" % u, 128, H); sb("mq%d" % u, 128, H)
-    sb("Dm", 128, I); sb("Bm", 128, I); sb("D12", 128, I); sb("pi", 2, I); sb("pk", 2, I); sb("rp", 256, I); sb("li", 256, I)
-    sb("crep", 256, U); sb("kf", 1, F); sb("pg", 1, F)
+    sb("Dm", 128, I); sb("Bm", 128, I); sb("pi", 2, I); sb("pk", 2, I); sb("rp", 256, I); sb("li", 256, I)
+    sb("crep", 256, U); sb("crep1", 16, U); sb("KH", 256, B); sb("KF", 256, B); sb("kf", 1, F); sb("pg", 1, F)
     sb("BO", 128, B); sb("BO16", 128, H); sb("BO5", 128, H); sb("BOn", 128, B)
-    sb("ID", 128, B); sb("E1", 128, B); sb("E2", 128, B); sb("OHM", 128, B); sb("DST", 128, B)
+    sb("ID", 128, B); sb("E1", 128, B); sb("E2", 128, B); sb("E3", 128, B); sb("OHM", 128, B); sb("DST", 128, B)
     sb("TRI", 128, B); sb("Z", 144, B); sb("ZM", 128, B)
     sb("cols", 16, F); sb("SR", 640, B); sb("SEL", 768, B); sb("ZT", 864, B)
     sb("rd", 256, F); sb("ta", 256, F); sb("tb", 256, F); sb("CMh", 256, B); sb("CMf", 256, B); sb("MX", 256, B)
@@ -70,7 +71,8 @@ def rank_program(g, core, T, topo):
     known = {e: {} for e in queue}
     free = {e: 0.0 for e in queue}
     snap, acc, when = {}, {}, {}
-    CY, WAKE, GA, SC = 0.83, 100.0, 1.5, 3.0
+    CY, WAKE, GA, SC = 0.83, 140.0, 1.5, 3.0
+    LAND = {"ld2": 8000.0, "ld4": 9000.0, "ld5": 10000.0, "ld6": 13000.0}
 
     def a(name, lo=None, hi=None, step=1, rows=128):
         name, base, cols = AT.get(name, (name, 0, 0))
@@ -134,6 +136,8 @@ def rank_program(g, core, T, topo):
                 acc[name] = keep
 
     def start(op):
+        if isinstance(op, list):
+            return max(start(o) for o in op)
         eng, call, reads, writes, dur = op[:5]
         t = free[eng]
         for s, v in needs(eng, reads, writes).items():
@@ -146,6 +150,10 @@ def rank_program(g, core, T, topo):
         when[tok] = t
 
     def do(op):
+        if isinstance(op, list):
+            for o in op:
+                do(o)
+            return
         eng, call, reads, writes, dur = op[:5]
         t = start(op)
         order(eng, reads, writes)
@@ -161,13 +169,19 @@ def rank_program(g, core, T, topo):
         done((s, count[s]), eng, t + dur)
         record(eng, (s, count[s]), reads, writes)
 
+    pool = []
+
+    def spawn(p, j):
+        pool.append([p, j, None])
+
     def together(jobs):
-        jobs = [[p, j, None] for p, j in jobs]
-        live = list(jobs)
+        live = pool
+        for p, j in jobs:
+            spawn(p, j)
         while live:
             best = None
             for x in list(live):
-                while not isinstance(x[2], tuple) and x[2] != "end":
+                while not isinstance(x[2], (tuple, list)) and x[2] != "end":
                     if x[2] is None:
                         x[2] = next(x[1], "end")
                     elif x[2]():
@@ -176,7 +190,7 @@ def rank_program(g, core, T, topo):
                         break
                 if x[2] == "end":
                     live.remove(x)
-                elif isinstance(x[2], tuple):
+                elif isinstance(x[2], (tuple, list)):
                     k = (start(x[2]), x[0])
                     if best is None or k < best[0]:
                         best = (k, x)
@@ -232,10 +246,16 @@ def rank_program(g, core, T, topo):
     def iota(out, pattern, base, ch):
         return ("G", lambda: g.iota(out[0], pattern, base, ch), [], out[1], 130.0 + 2 * out[2] * CY)
 
+    def zeros(out):
+        return ("G", lambda: g.iota(out[0], [[0, out[2]]], 0, 0, allow_small_or_imprecise_dtypes=True), [], out[1], 130.0 + 2 * out[2] * CY)
+
+    def sel(out, in_, pattern, base, ch):
+        return ("G", lambda: g.affine_select(out[0], in_[0], pattern, OP.is_equal, 0.0, base, ch), regs_of(in_), out[1], 170.0 + 2 * out[2] * CY)
+
     def load(eng, sem, out, src, reg):
         order(eng, [], reg)
         queue[eng].dma_start(out, src).then_inc(T.sem[sem], 16)
-        done((sem, 16), eng, 3000.0 + 1500.0 * (SCRATCH[reg[0][0]][1][1] > 1000))
+        done((sem, 16), eng, LAND.get(sem, 3000.0))
         record("D" + sem, (sem, 16), [], reg)
 
     def send(r, src, dst, sem, lsem):
@@ -284,9 +304,9 @@ def rank_program(g, core, T, topo):
         yield iota(a("li"), [[1, 256]], 0, 0)
         yield iota(a("pi"), [[0, 2]], 0, 1)
         yield iota(a("Bm"), [[1, 8], [0, 16]], 0, 0)
-        yield iota(a("Dm"), [[1, 128]], 0, -1)
-        yield iota(a("D12"), [[-12, 8], [0, 16]], 0, 1)
         yield iota(a("rp"), [[0, 16], [1, 16]], 0, 0)
+        yield iota(a("Dm"), [[1, 128]], 0, -1)
+        yield fill(a("ONE"), 1.0)
         yield cp(a("crep"), a("li"))
         yield cp(a("nU1"), a("n0_i"))
         yield ts(a("pk", 0, 1), a("pi", 0, 1), 15, OP.bitwise_and)
@@ -295,6 +315,7 @@ def rank_program(g, core, T, topo):
         yield cp(a("pg"), a("pk", 1, 2))
         yield fill(col(3), BETA)
         yield fill(col(14), 1.0)
+        yield fill(col(15), -1.0)
         yield ts(a("BO"), a("Bm"), a("pg"), OP.is_equal)
         yield fill(a("Z"), 0.0)
         yield cp(a("Z", 15, 143, 16), a("BO", 0, 128, 16))
@@ -304,15 +325,13 @@ def rank_program(g, core, T, topo):
         yield ts(a("BO5"), a("BO"), 5.0, OP.mult)
         yield ts(a("rd"), a("rp"), kf, OP.subtract)
         yield ts(a("MX"), a("rd"), 0.0, OP.is_equal)
-        yield ts(a("ID"), a("Dm"), 0, OP.is_equal)
         yield ts(a("TRI"), a("Dm"), 0, OP.is_ge, 64.0, OP.mult)
         yield tt(a("TRI"), a("TRI"), a("BO"), OP.mult)
         yield fill(a("TRI", 15, 128, 16), 0.0)
         yield ts(col(0), kf, 15.0, OP.is_lt)
-        yield ts(a("E1"), a("Dm"), 1, OP.is_equal)
-        yield ts(a("E2"), a("Dm"), -15, OP.is_equal)
-        yield tt(a("E1"), a("E1"), a("E2"), OP.add)
-        yield tt(a("E1"), a("E1"), a("BO"), OP.mult)
+        yield fill(a("SIX"), 0.0625)
+        yield mark("o")
+        yield tt(a("E1"), a("E1"), a("E3"), OP.add)
         yield ts(a("E2"), a("ID"), col(0), OP.mult)
         yield tt(a("OHM"), a("E1"), a("E2"), OP.subtract)
         yield ts(col(1), kf, -EPS, OP.mult)
@@ -321,35 +340,29 @@ def rank_program(g, core, T, topo):
         yield cp(a("drb", rows=96), a("dr_i", rows=96))
         yield ts(a("w_i", rows=96), a("dr_i", rows=96), 15, OP.bitwise_and)
         yield cp(a("wb", rows=96), a("w_i", rows=96))
-        for j in range(6):
-            yield ts(a("SEL", 128 * j, 128 * j + 128, rows=96), a("D12", rows=96), home_te[j], OP.is_equal)
         yield ts(a("y1"), a("rch_s"), -1.0, OP.add)
         yield ts(a("pre1"), a("n0_i"), 13.0, OP.mult, 1.0 + 10240.0, OP.add)
         for x in draws(0):
             yield x
-        for n, c in ([("DST", 0.0), ("ZT", 0.0), ("ONE", 1.0), ("SIX", 0.0625), ("send", 0.0)]):
-            yield fill(a(n), c)
-        for d in range(4):
-            yield tt(a("DST", d, 128, 16), a("OHM", d, 128, 16), a("OHM", d + 4, 128, 16), OP.add)
-            yield tt(a("DST", d, 128, 16), a("DST", d, 128, 16), a("OHM", d + 8, 128, 16), OP.add)
-            yield tt(a("DST", d, 128, 16), a("DST", d, 128, 16), a("OHM", d + 12, 128, 16), OP.add)
+        yield tt(a("DST", 0, 116), a("OHM", 0, 116), a("OHM", 4, 120), OP.add)
+        yield tt(a("E1", 0, 116), a("OHM", 8, 124), a("OHM", 12, 128), OP.add)
+        yield ts(a("E2"), a("rp", 0, 128), 4, OP.is_lt)
+        yield tt(a("DST", 0, 116), a("DST", 0, 116), a("E1", 0, 116), OP.add)
+        yield tt(a("DST", 0, 116), a("DST", 0, 116), a("E2", 0, 116), OP.mult)
         yield ts(col(4), kf, 320.0, OP.mult, -1.0, OP.add)
         yield ts(col(5), kf, 320.0, OP.mult, 64.0, OP.add)
         yield ts(col(6), kf, 4096.0, OP.add)
-        for j in range(6):
-            yield ts(a("ZT", 144 * j + 15, 144 * j + 143, 16, rows=96), a("D12", 0, 128, 16, rows=96), far_te[j], OP.is_equal)
+        yield mark("z")
         for x in aux_static(0):
             yield x
         marks["c"] = 1
         yield ts(col(7), kf, 2.0, OP.is_equal)
-        yield ts(col(8), kf, 3.0, OP.is_equal, 256.0, OP.mult)
+        yield ts(col(8), kf, 3.0, OP.is_equal)
         yield tt(col(7), col(7), col(8), OP.add)
         yield ts(a("BOn"), a("BO"), col(7), OP.mult)
         for j, (row, w) in enumerate(((0, 1.0), (1, 1.0), (5, 1.0), (6, 1.0), (4, -8192.0))):
             yield ts(col(9 + j), kf, float(row), OP.is_equal, w, OP.mult)
             yield ts(a("SR", 128 * j, 128 * j + 128), a("BO"), col(9 + j), OP.mult)
-        for t in range(RO):
-            yield fill(a("zr%d" % t), 0.0)
         yield ts(a("ZM"), a("ID"), 16.0, OP.mult)
         yield tt(a("ZM"), a("ZM"), a("BO"), OP.subtract)
         yield ts(a("ta"), a("rd"), 0.0, OP.is_gt, 16384.0, OP.mult)
@@ -358,7 +371,30 @@ def rank_program(g, core, T, topo):
         yield ts(a("CMh"), a("ta"), 2048.0, OP.add)
         yield ts(a("CMf"), a("ta"), 10240.0, OP.add)
         yield ts(a("RST"), a("rp"), 0, OP.is_gt)
+        yield ts(a("crep1"), a("li", 0, 16), 1.0, OP.add)
+        yield ts(col(8), kf, 4112.0, OP.add)
+        yield fill(a("KH"), 2048.0)
+        yield fill(a("KF"), 10240.0)
+        yield act(a("paym"), a("pay_s"), ACT.Identity, bias=col(15))
         marks["e"] = 1
+
+    def patterns():
+        for j in (0, 1):
+            yield sel(a("SEL", 128 * j, 128 * j + 128, rows=96), a("ONE", 0, 128, rows=96), [[-12, 8], [0, 16]], -home_te[j], 1)
+        yield sel(a("ID"), a("ONE", 0, 128), [[-1, 128]], 0, 1)
+        yield sel(a("E1"), a("BO"), [[1, 128]], -1, -1)
+        yield sel(a("E3"), a("BO"), [[1, 128]], 15, -1)
+        yield zeros(a("DST"))
+        marks["o"] = 1
+        yield zeros(a("ZT"))
+        for j in range(6):
+            yield sel(a("ZT", 144 * j + 15, 144 * j + 143, 16, rows=96), a("ONE", 0, 8, rows=96), [[-12, 8]], -far_te[j], 1)
+        marks["z"] = 1
+        yield zeros(a("send"))
+        for t in range(RO):
+            yield zeros(a("zr%d" % t))
+        for j in range(2, 6):
+            yield sel(a("SEL", 128 * j, 128 * j + 128, rows=96), a("ONE", 0, 128, rows=96), [[-12, 8], [0, 16]], -home_te[j], 1)
 
     def draws(t):
         for src, b in (("drb", "b6"), ("wb", "b7")):
@@ -372,10 +408,11 @@ def rank_program(g, core, T, topo):
         marks["v%d" % t] = 1
 
     def aux_static(t):
+        grp = []
         for k, (src, j, row) in enumerate((("drb", 0, 0), ("drb", 1, 1), ("wb", 0, 5), ("wb", 1, 6))):
             s = 144 * (2 * t + j) + 15 - row
-            yield mm(a("b7", 0, 256), a("ZT", s, s + 128, rows=96), a(src, rows=96), k == 0, False)
-        yield mm(a("b7", 0, 256), a("Z", 11, 139), a("SIX"), False, True)
+            grp.append(mm(a("b7", 0, 256), a("ZT", s, s + 128, rows=96), a(src, rows=96), k == 0, False))
+        yield grp + [mm(a("b7", 0, 256), a("Z", 11, 139), a("SIX"), False, True)]
         yield act(a("auxS%d" % t), a("b7", 0, 256), ACT.Copy)
         marks["x%d" % t] = 1
 
@@ -426,36 +463,48 @@ def rank_program(g, core, T, topo):
         yield tt(a("t1", lo, hi), a(bank, n, 2 * n), a(vb, at + lo, at + hi), OP.mult)
         yield tt(a("ind", lo, hi), a(bank, 2 * n, 3 * n), a("t1", lo, hi), OP.is_lt)
         yield mm(a(bank, 3 * n, 4 * n), a("OHM"), a("ind", lo, hi))
-        if e == 2:
-            yield mark("c")
+
+        def slots():
             yield mm(a("b4", lo, hi), a("DST"), a("ind", lo, hi))
-        yield tt(a("q%d" % e, lo, hi), a(bank, 3 * n, 4 * n), a("Ah%d" % e, lo, hi), OP.mult)
-        for o in diag(bank, 0, "q%d" % e, "BO16", "mk%d" % u, bank, n, "BO5", n, lo, hi):
-            yield o
-        if e == 2:
             yield lambda: lo == 0 or "s%d_%d" % (t, lo) in marks
             yield scan(a("cum", lo, hi), a("ONE", lo, hi), a("b4", lo, hi), col(4) if lo == 0 else a("cum", lo - 1, lo))
             marks["s%d_%d" % (t, hi)] = 1
             yield tt(a("Q", lo, hi), a("b4", lo, hi), a("cum", lo, hi), OP.mult)
             for o in diag("b5", 128 * u, "Q", "BO16", "mq%d" % u, "b4", 256 + tl, "BO16", n, lo, hi):
                 yield o
-        p = a(bank, n, n + n // 16)
+            yield cp(a("slot", tl, th), a("b4", 256 + tl, 256 + th))
+            marks["S%d_%d" % (t, u)] = 1
         if e == 2:
-            yield tt(a("s_i", tl, th), p, a("pre%d" % e, tl, th), OP.add)
+            yield mark("c")
+            spawn(u + 0.2, slots())
+        if e in (2, 4):
+            yield mark("R%d_%d_%d" % (t, e, u))
+        yield tt(a("q%d" % e, lo, hi), a(bank, 3 * n, 4 * n), a("Ah%d" % e, lo, hi), OP.mult)
+        for o in diag(bank, 0, "q%d" % e, "BO16", "mk%d" % u, bank, n, "BO5", n, lo, hi):
+            yield o
+        p = a(bank, n, n + n // 16)
         yield ts(a("rec%d" % e, tl, th), p, 0.2, OP.mult, 2048.25, OP.add)
-        yield tt(a(YO[e], lo, hi), via(a("P"), a("rec%d" % e, tl, th)), a(YN[e], lo, hi), OP.min)
-        if e in (1, 3):
-            for o in spread(e + 1, lo, hi):
-                yield o
-        if e != 2:
-            yield tt(a("s_i", tl, th), p, a("pre%d" % e, tl, th), OP.add)
+
+        def reaches():
+            yield tt(a(YO[e], lo, hi), via(a("P"), a("rec%d" % e, tl, th)), a(YN[e], lo, hi), OP.min)
+            if e in (1, 3):
+                for o in spread(e + 1, lo, hi):
+                    yield o
+            marks["Y%d_%d_%d" % (t, e, u)] = 1
+        spawn(u - 0.5, reaches())
+        yield tt(a("s_i", tl, th), p, a("pre%d" % e, tl, th), OP.add)
         yield ts(a("n_i", tl, th), a("s_i", tl, th), 2047, OP.bitwise_and)
         if e != 2:
             yield cp(a("nU%d" % (e + 1), tl, th), a("n_i", tl, th))
         if e in (1, 3):
             yield acts_at(e + 1, lo, hi)
-            yield ts(a("pre%d" % (e + 1), tl, th), a("n_i", tl, th), 13.0, OP.mult, e + 1.0 + 10240.0, OP.add)
-            yield acts_half(e + 1, lo, hi)
+
+            def rest():
+                yield ts(a("pre%d" % (e + 1), tl, th), a("n_i", tl, th), 13.0, OP.mult, e + 1.0 + 10240.0, OP.add)
+                yield acts_half(e + 1, lo, hi)
+                marks["R%d_%d_%d" % (t, e + 1, u)] = 1
+            spawn(u + 5, rest())
+        yield mark("Y%d_%d_%d" % (t, e, u))
 
     def home(t, u, lo, hi):
         tl, th = lo // 16, hi // 16
@@ -466,24 +515,25 @@ def rank_program(g, core, T, topo):
         for e in (1, 2):
             for o in level(e, t, u, lo, hi):
                 yield o
-        yield ts(a("nlh", tl, th), a("n_i", tl, th), 255, OP.bitwise_and)
-        yield ts(a("nlh", 16 + tl, 16 + th), a("n_i", tl, th), 8, OP.arith_shift_right)
-        yield cp(a("slot", tl, th), a("b4", 256 + tl, 256 + th))
-        yield cp(a("nlf", tl, th), a("nlh", tl, th))
-        yield cp(a("nlf", 16 + tl, 16 + th), a("nlh", 16 + tl, 16 + th))
-        yield tt(a("nx", lo, hi), via(a("nlf", 0, 16), a("crep", tl, th)), a("MX", lo, hi), OP.mult)
-        yield tt(a("nx", 256 + lo, 256 + hi), via(a("nlf", 16, 32), a("crep", tl, th)), a("MX", lo, hi), OP.mult)
+        n = hi - lo
+        w = n // 16
+        f0, x0 = 16 * u, 256 * u
+        yield cp(a("nlf", f0, f0 + w), a("n_i", tl, th))
+        yield tt(a("nlf", f0 + w, f0 + 2 * w), a("n_i", tl, th), a("nlf", f0, f0 + w), OP.subtract)
+        yield tt(a("nx", x0, x0 + 2 * n), via(a("nlf", f0, f0 + 2 * w), a("crep", 0, 2 * w)), a("MX", 0, 2 * n), OP.mult)
         yield mark("x%d" % t)
-        yield mm(a("b6", lo, hi), a("ID"), a("auxS%d" % t, lo, hi), True, False)
-        yield mm(a("b6", lo, hi), a("Z", 13, 141), a("nx", lo, hi), False, False)
-        yield mm(a("b6", lo, hi), a("Z", 12, 140), a("nx", 256 + lo, 256 + hi), False, True)
+        yield [mm(a("b6", lo, hi), a("ID"), a("auxS%d" % t, lo, hi), True, False),
+               mm(a("b6", lo, hi), a("Z", 13, 141), a("nx", x0, x0 + n), False, False),
+               mm(a("b6", lo, hi), a("Z", 12, 140), a("nx", x0 + n, x0 + 2 * n), False, True)]
         yield act(a("auxB", lo, hi), a("b6", lo, hi), ACT.Copy)
+        yield mark("S%d_%d" % (t, u))
         yield scatter(a("send", 0, 1216), a("slot", tl, th), a("y3", lo, hi))
         marks["y%d_%d" % (t, lo)] = 1
         yield lambda: all("y%d_%d" % (t, l) in marks for l, h in HUN)
         yield scatter(a("send", 64, 1280), a("slot", tl, th), a("auxB", lo, hi))
 
     def depart(t):
+        order("G", [("zr%d" % t, 0, 1280)], [])
         for r in others:
             do(send(r, a("send", REG * r, REG * r + 128), T["land%d" % t][:, 128 * me:128 * me + 128], "a%d_%d" % (t, me), "la%d_%d" % (t, r)))
         for i, r in enumerate(others):
@@ -514,8 +564,8 @@ def rank_program(g, core, T, topo):
         for e in (3, 4):
             for o in level(e, t, u, lo, hi):
                 yield o
-        yield act(a("x5", lo, hi), a("yF5", lo, hi), ACT.Identity, bias=col(14))
-        yield tt(a("lv", lo, hi), via(a("pay_s"), a("nU5", tl, th)), a("x5", lo, hi), OP.min)
+        marks["g%d_%d" % (t, u)] = 1
+        yield tt(a("lv", lo, hi), via(a("paym"), a("nU5", tl, th)), a("yF5", lo, hi), OP.min)
         yield mm(a(bank, 0, n), a("ZM"), a("lv", lo, hi))
         yield act(a("zF", lo, hi), a(bank, 0, n), ACT.Sign)
         for p in ps:
@@ -528,45 +578,54 @@ def rank_program(g, core, T, topo):
         yield ts(a("NV", lo, hi), a("NV", lo, hi), 15.0, OP.min, -15.0, OP.max)
         marks["f%d_%d" % (t, u)] = 1
 
-    def first_of(n, q, cm, extra, rec):
+    def first_of(n, q, cm, kc, extra, rec):
+        b = "b7" if n == "h" else "b6"
         yield ts(a("rf8" + n), a(rec), 2.0 ** -13, OP.mult)
-        yield mm(a("b7", 0, 256), a("BO16"), a(q), True, False)
-        yield mm(a("b7", 0, 256), a("ID"), a(cm), False, False)
-        yield mm(a("b7", 0, 256), extra[0], extra[1], False, True)
+        yield [mm(a(b, 0, 256), a("BO16"), a(q), True, False), mm(a(b, 0, 256), a("ID"), a(cm), False, False),
+               mm(a(b, 0, 256), extra[0], extra[1], False, True)]
+        yield [mm(a(b, 256, 512), a("BO16"), a(q), True, False), mm(a(b, 256, 512), a("ID"), a(kc), False, False),
+               mm(a(b, 256, 512), extra[0], extra[1], False, True)]
         yield act(a("Y" + n), via(a("rf8" + n), a("crep", 0, 16)), ACT.Copy, scale=8192.0)
-        yield tt(a("eq" + n), a("b7", 0, 256), a("Y" + n), OP.is_equal)
+        yield act(a("Z2" + n, 0, 240), via(a("rf8" + n), a("crep1", 0, 15)), ACT.Copy, scale=8192.0)
+        yield tt(a("eq" + n), a(b, 0, 256), a("Y" + n), OP.is_equal)
         yield scan(a("lc" + n), a("RST"), a("eq" + n), 0.0)
+        yield tt(a("er" + n, 0, 240), a(b, 256, 496), a("Z2" + n, 0, 240), OP.is_equal)
         yield tt(a("u" + n), a("lc" + n, 15, 256, 16), a("rf8" + n), OP.add)
-        yield ts(a("off" + n, 0, 32, 2), a("u" + n), 8192.0, OP.mult, col(6), OP.min)
+        yield scan(a("ld" + n, 0, 240), a("RST", 0, 240), a("er" + n, 0, 240), 0.0)
+        yield ts(a("off" + n, 0, 16, 2), a("u" + n, 0, 16, 2), 8192.0, OP.mult, col(6), OP.min)
+        yield tt(a("u" + n, 1, 16, 2), a("u" + n, 1, 16, 2), a("ld" + n, 15, 240, 32), OP.add)
+        yield ts(a("off" + n, 1, 16, 2), a("u" + n, 1, 16, 2), 8192.0, OP.mult, col(8), OP.min)
 
     def change(n, blocks, values):
         for c in blocks:
-            yield scatter(a("regs_s"), a("off" + n, 2 * c, 2 * c + 1), a(values, 16 * c, 16 * c + 16))
+            yield scatter(a("regs_s"), a("off" + n, 2 * c, 2 * c + 2), a(values, 32 * c, 32 * c + 32))
 
     def waiting(t):
         yield mark("e")
         yield ts(a("ng"), a("Q"), col(5), OP.is_ge, 8192.0, OP.mult)
-        for o in first_of("h", "q2", "CMh", (a("BO"), a("ng")), "rec2"):
+        for o in first_of("h", "q2", "CMh", "KH", (a("BO"), a("ng")), "rec2"):
             yield o
         if t + 1 < RO:
+            yield zeros(a("send"))
             for o in draws(t + 1):
                 yield o
             for o in aux_static(t + 1):
                 yield o
 
     def leaves(t):
+        yield lambda: all("g%d_%d" % (t, u) in marks for u in range(len(FUN)))
+        for o in first_of("f", "q4", "CMf", "KF", (a("SR", 512, 640), a("auxF")), "rec4"):
+            yield o
         yield lambda: all("f%d_%d" % (t, u) in marks for u in range(len(FUN)))
-        for o in first_of("f", "q4", "CMf", (a("SR", 512, 640), a("auxF")), "rec4"):
+        for o in change("f", [2 * place.index(r) + c for r in (3, 2, 1, 0) for c in (1, 0)], "NV"):
             yield o
-        for o in change("f", [4 * place.index(r) + c for r in (3, 2, 1, 0) for c in (3, 2, 1, 0)], "NV"):
-            yield o
-        if t + 1 < RO:
-            yield fill(a("send"), 0.0)
-        for lo in range(0, 256, 64):
-            yield act(a("zl", lo, lo + 64), via(a("zr%d" % t), a("slot", lo // 16, lo // 16 + 4)), ACT.Copy, scale=-1.0)
-        yield tt(a("HV"), via(a("regs_s", 0, 4096), a("rec2")), a("zl"), OP.add)
-        yield ts(a("HV"), a("HV"), 15.0, OP.min, -15.0, OP.max)
-        for o in change("h", list(range(15, -1, -1)), "HV"):
+        for lo in (128, 0):
+            yield act(a("zl", lo, lo + 128), via(a("zr%d" % t), a("slot", lo // 16, lo // 16 + 8)), ACT.Copy, scale=-1.0)
+        for lo in (128, 0):
+            yield tt(a("HV", lo, lo + 128), via(a("regs_s", 0, 4096), a("rec2", lo // 16, lo // 16 + 8)), a("zl", lo, lo + 128), OP.add)
+        for lo in (128, 0):
+            yield ts(a("HV", lo, lo + 128), a("HV", lo, lo + 128), 15.0, OP.min, -15.0, OP.max)
+        for o in change("h", list(range(7, -1, -1)), "HV"):
             yield o
 
     for t in range(RO):
@@ -575,7 +634,7 @@ def rank_program(g, core, T, topo):
             c = constants()
             for i in range(17):
                 do(next(c))
-            together([(9, c), (8, relu_records())] + jobs)
+            together([(9, c), (8, relu_records()), (9, patterns())] + jobs)
         else:
             for o in relu_records():
                 do(o)
@@ -583,7 +642,7 @@ def rank_program(g, core, T, topo):
         depart(t)
         together([(u, far(t, u, FU[u], lo, hi)) for u, (lo, hi) in enumerate(FUN)] + [(8, waiting(t)), (7, leaves(t))])
 
-    order("Y", [("regs_s", 0, 4112)], [])
+    order("Y", [("regs_s", 0, 4128)], [])
     g.sync.dma_start(T.yr[:], T.regs_s[:, 0:4096]).then_inc(T.sem.yo, 16)
     g.sync.wait_ge(T.sem.yo, 16)
     for s in ("eV", "eP", "eS", "eG"):

from concourse.bass import DstId, RemoteDMATransfer
from concourse.mybir import dt, AluOpType, AxisListType, ActivationFunctionType

N = 4
RO = 3
REG = 320
EPS = 2.0 ** -30
BETA = 2.0 ** -12
HU = (128, 128)
FU = ((0,), (1, 2), (3,))
CG, CW, CS = 64, 64, 64

F, B, H, I, U = "float32", "bfloat16", "float16", "int32", "uint16"


def _scratch():
    s, at = {}, {}
    def sb(name, cols, d):
        if cols > 1024 or name in ("rch_s", "n0_i", "dr_i") or name[:4] == "land":
            s[name] = ("sbuf", [128, cols], d)
        else:
            big = "p" + d
            lo = s[big][1][1] if big in s else 0
            s[big] = ("sbuf", [128, lo + cols + -cols % 32], d)
            at[name] = (big, lo, cols)
    sb("acts_i", 2048, I); sb("regs_s", 4128, B); sb("P", 4096, B); sb("pay_s", 2048, B); sb("paym", 2048, B)
    sb("rch_s", 256, B); sb("n0_i", 16, I); sb("dr_i", 256, I); sb("w_i", 256, I)
    sb("drb", 256, B); sb("wb", 256, B)
    sb("xr1", 4096, B); sb("xr", 4096, B); sb("W", 4096, B)
    for e in (1, 2, 3, 4):
        sb("A%d" % e, 256, U); sb("Ah%d" % e, 256, H); sb("q%d" % e, 256, H); sb("rec%d" % e, 16, U); sb("pre%d" % e, 16, F)
    for e in (1, 2, 3, 4, 5):
        sb("nU%d" % e, 16, U)
    for n in ("y1", "y2", "y3", "yF3", "yF4", "yF5", "lv", "zF", "NV", "zl", "HV", "ms", "ind", "auxB", "auxF", "ng"):
        sb(n, 256, B)
    sb("t1", 256, F); sb("s_i", 16, I); sb("n_i", 16, I); sb("nlf", 64, B); sb("nx", 1024, B)
    for t in range(RO):
        sb("vb%d" % t, 512, F); sb("wt%d" % t, 512, B); sb("auxS%d" % t, 256, B); sb("land%d" % t, 512, B); sb("zr%d" % t, 1280, B)
    sb("vbF", 512, F); sb("wtF", 512, B)
    sb("cum", 256, F); sb("Q", 256, H); sb("slot", 16, U); sb("send", 1280, B)
    for n in ("h", "f"):
        sb("rf8" + n, 16, F); sb("Y" + n, 256, F); sb("eq" + n, 256, B); sb("lc" + n, 256, B); sb("u" + n, 16, F)
        sb("off" + n, 16, U); sb("Z2" + n, 256, F); sb("er" + n, 256, B); sb("ld" + n, 256, B)
    for u in range(4):
        sb("mk%d" % u, 128, H); sb("mq%d" % u, 128, H)
    sb("Dm", 128, I); sb("Bm", 128, I); sb("pi", 2, I); sb("pk", 2, I); sb("rp", 256, I); sb("li", 256, I)
    sb("crep", 256, U); sb("crep1", 16, U); sb("KH", 256, B); sb("KF", 256, B); sb("kf", 1, F); sb("pg", 1, F)
    sb("BO", 128, B); sb("BO16", 128, H); sb("BO5", 128, H); sb("BOn", 128, B)
    sb("ID", 128, B); sb("E1", 128, B); sb("E2", 128, B); sb("E3", 128, B); sb("OHM", 128, B); sb("DST", 128, B)
    sb("TRI", 128, B); sb("Z", 144, B); sb("ZM", 128, B)
    sb("cols", 16, F); sb("SR", 640, B); sb("SEL", 768, B); sb("ZT", 864, B)
    sb("rd", 256, F); sb("ta", 256, F); sb("tb", 256, F); sb("CMh", 256, B); sb("CMf", 256, B); sb("MX", 256, B)
    sb("RST", 256, B); sb("ONE", 256, B); sb("SIX", 256, B)
    for b in range(8):
        s["b%d" % b] = ("psum", [128, 512], F)
    return s, at


SCRATCH, AT = _scratch()
SEMAPHORES = (["eV", "eP", "eS", "eG"] + ["ld%d" % i for i in range(8)] + ["yo"]
              + ["%s%d_%d" % (k, t, r) for k in ("a", "z", "la", "lz") for t in range(RO) for r in range(N)])


def rank_program(g, core, T, topo):
    me = T.rank_of(core)
    if me is None:
        return
    OP, ACT = AluOpType, ActivationFunctionType
    queue = {"V": g.vector, "P": g.tensor, "S": g.scalar, "G": g, "Y": g.sync}
    count = {"eV": 0, "eP": 0, "eS": 0, "eG": 0}
    known = {e: {} for e in queue}
    free = {e: 0.0 for e in queue}
    snap, acc, when = {}, {}, {}
    CY, WAKE, GA, SC = 0.83, 140.0, 1.5, 3.0
    LAND = {"ld2": 8000.0, "ld4": 9000.0, "ld5": 10000.0, "ld6": 13000.0}

    def a(name, lo=None, hi=None, step=1, rows=128):
        name, base, cols = AT.get(name, (name, 0, 0))
        t = T[name]
        if lo is None:
            lo, hi = 0, cols or SCRATCH[name][1][1]
        lo, hi = base + lo, base + hi
        ap = t[0:rows, lo:hi] if step == 1 else t[0:rows, lo:hi:step]
        return ap, [(name, lo, hi)], (hi - lo + step - 1) // step, 0

    def via(win, off):
        return win[0].indirect(off[0]), win[1] + off[1], 16 * off[2], 1

    def narrow(x):
        return SCRATCH[x[1][0][0]][2] in (B, U, H)

    def merge(eng, tok):
        k = known[eng]
        for s, v in list(snap.get(tok, {}).items()) + [tok]:
            if k.get(s, 0) < v:
                k[s] = v

    def needs(eng, reads, writes):
        need = {}
        for regs, w in ((reads, False), (writes, True)):
            for name, lo, hi in regs:
                bank = SCRATCH[name][0] == "psum"
                for (e2, tok, l2, h2, w2) in acc.get(name, []):
                    if bank and e2 != eng:
                        hit = True
                    elif l2 < hi and lo < h2:
                        if w and w2:
                            hit = not (eng == "P" and e2 == "P")
                        elif w:
                            hit = e2 != eng
                        else:
                            hit = w2
                    else:
                        hit = False
                    if hit and known[eng].get(tok[0], 0) < tok[1] and need.get(tok[0], 0) < tok[1]:
                        need[tok[0]] = tok[1]
        return need

    def order(eng, reads, writes):
        need = needs(eng, reads, writes)
        for s in sorted(need):
            v = need[s]
            if any(s2 != s and snap.get((s2, need[s2]), {}).get(s, 0) >= v for s2 in need):
                need[s] = 0
        for s in sorted(need):
            if need[s]:
                queue[eng].wait_ge(T.sem[s], need[s])
                merge(eng, (s, need[s]))

    def record(eng, tok, reads, writes):
        for regs, w in ((reads, False), (writes, True)):
            for name, lo, hi in regs:
                old = acc.get(name, [])
                keep = [x for x in old if not (lo <= x[2] and x[3] <= hi and (w or (x[0] == eng and not x[4])))]
                keep.append((eng, tok, lo, hi, w))
                acc[name] = keep

    def start(op):
        if isinstance(op, list):
            return max(start(o) for o in op)
        eng, call, reads, writes, dur = op[:5]
        t = free[eng]
        for s, v in needs(eng, reads, writes).items():
            t = max(t, when.get((s, v), 0.0) + WAKE)
        return t

    def done(tok, eng, t):
        sn = dict(known[eng]); sn[tok[0]] = tok[1]
        snap[tok] = sn
        when[tok] = t

    def do(op):
        if isinstance(op, list):
            for o in op:
                do(o)
            return
        eng, call, reads, writes, dur = op[:5]
        t = start(op)
        order(eng, reads, writes)
        free[eng] = t + dur
        if len(op) > 5:
            call()
            done(op[5], eng, t + 3000.0)
            record("R" + op[5][0], op[5], reads, [])
            return
        s = "e" + eng
        count[s] += 1
        call().then_inc(T.sem[s], 1)
        done((s, count[s]), eng, t + dur)
        record(eng, (s, count[s]), reads, writes)

    pool = []

    def spawn(p, j):
        pool.append([p, j, None])

    def together(jobs):
        live = pool
        for p, j in jobs:
            spawn(p, j)
        while live:
            best = None
            for x in list(live):
                while not isinstance(x[2], (tuple, list)) and x[2] != "end":
                    if x[2] is None:
                        x[2] = next(x[1], "end")
                    elif x[2]():
                        x[2] = None
                    else:
                        break
                if x[2] == "end":
                    live.remove(x)
                elif isinstance(x[2], (tuple, list)):
                    k = (start(x[2]), x[0])
                    if best is None or k < best[0]:
                        best = (k, x)
            if best:
                do(best[1][2])
                best[1][2] = None

    def regs_of(*xs):
        return [r for x in xs if isinstance(x, tuple) for r in x[1]]

    def val(x):
        return x[0] if isinstance(x, tuple) else x

    def vop(call, out, ins, n, wide=1.0):
        x = [i for i in ins if i[3]]
        d = x[0][2] * GA * CY if x else out[2] * SC * CY if out[3] else max(64.0, n * wide) * CY
        return ("V", call, regs_of(*ins), out[1], 60.0 + d)

    def ts(out, in0, s1, op0, s2=None, op1=None):
        if op1 is None:
            f = lambda: g.vector.tensor_scalar(out[0], in0[0], val(s1), None, op0)
        else:
            f = lambda: g.vector.tensor_scalar(out[0], in0[0], val(s1), val(s2), op0, op1)
        return vop(f, out, [in0] + [x for x in (s1, s2) if isinstance(x, tuple)], in0[2], 0.5 if narrow(out) and narrow(in0) else 1.0)

    def tt(out, in0, in1, op):
        ps = any(SCRATCH[x[1][0][0]][0] == "psum" for x in (in0, in1))
        return vop(lambda: g.vector.tensor_tensor(out[0], in0[0], in1[0], op), out, [in0, in1], in1[2], 1.0 if ps else 2.0)

    def cp(out, in_):
        return vop(lambda: g.vector.tensor_copy(out[0], in_[0]), out, [in_], in_[2])

    def scatter(win, off, in_):
        return vop(lambda: g.vector.tensor_copy(win[0].indirect(off[0]), in_[0]), (None, win[1], in_[2], 1), [in_, off], in_[2])

    def fill(out, c):
        return vop(lambda: g.vector.memset(out[0], c), out, [], out[2], 0.5)

    def scan(out, d0, d1, init):
        return vop(lambda: g.vector.tensor_tensor_scan(out[0], d0[0], d1[0], val(init), OP.mult, OP.add), out,
                   [d0, d1] + [x for x in (init,) if isinstance(x, tuple)], d1[2], 0.5 if narrow(out) and narrow(d1) else 1.0)

    def act(out, in_, func, bias=0.0, scale=1.0):
        if func == ACT.Copy:
            f = lambda: g.scalar.activation(out[0], in_[0], func, scale=scale)
        else:
            f = lambda: g.scalar.activation(out[0], in_[0], func, bias=val(bias), scale=scale)
        return ("S", f, regs_of(in_, bias), out[1], 65.0 + in_[2] * GA * CY if in_[3] else 165.0 + in_[2] * CY)

    def mm(out, lhsT, rhs, start=True, stop=True):
        return ("P", lambda: g.tensor.matmul(out[0], lhsT[0], rhs[0], start, stop), regs_of(lhsT, rhs), out[1], 10.0 + max(64, rhs[2]) * CY)

    def iota(out, pattern, base, ch):
        return ("G", lambda: g.iota(out[0], pattern, base, ch), [], out[1], 130.0 + 2 * out[2] * CY)

    def zeros(out):
        return ("G", lambda: g.iota(out[0], [[0, out[2]]], 0, 0, allow_small_or_imprecise_dtypes=True), [], out[1], 130.0 + 2 * out[2] * CY)

    def sel(out, in_, pattern, base, ch):
        return ("G", lambda: g.affine_select(out[0], in_[0], pattern, OP.is_equal, 0.0, base, ch), regs_of(in_), out[1], 170.0 + 2 * out[2] * CY)

    def load(eng, sem, out, src, reg):
        order(eng, [], reg)
        queue[eng].dma_start(out, src).then_inc(T.sem[sem], 16)
        done((sem, 16), eng, LAND.get(sem, 3000.0))
        record("D" + sem, (sem, 16), [], reg)

    def send(r, src, dst, sem, lsem):
        rid, pid, _ = topo.addr(T.cores[r])
        m = sum(1 << x for x in topo.engines(core, T.cores[r])[:8])
        return ("G", lambda: g.remote_dma(dst, src[0], T.sem[sem], T.sem[lsem], pid, rid, m), regs_of(src), [], 300.0, (lsem, 8))

    def arrives(sem, regions, t):
        snap[(sem, 8)] = {sem: 8}
        when[(sem, 8)] = t
        record("R" + sem, (sem, 8), [], regions)

    def far_key(r):
        c1, c2 = topo.chip(core), topo.chip(T.cores[r])
        return 0 if topo.mates(c1, c2) else 1 if topo.same_plane(c1, c2) else 2
    others = sorted([r for r in range(N) if r != me], key=far_key)
    place = [me] + others
    def units(sizes):
        out, lo = [], 0
        for n in sizes:
            out.append((lo, lo + n))
            lo += n
        return out
    HUN = units(HU)
    FUN = units([64 * len(p) for p in FU])

    load("Y", "ld0", T.n0_i[:], T.n0[:], [("n0_i", 0, 16)])
    load("S", "ld1", T.rch_s[:], T.rch[:], [("rch_s", 0, 256)])
    load("Y", "ld2", T.acts_i[:], T.acts[:], [("acts_i", 0, 2048)])
    load("S", "ld3", T.dr_i[0:96, :], T.dr[:, :], [("dr_i", 0, 256)])
    load("S", "ld4", T.regs_s[:, 0:2048], T.regs[:, 0:2048], [("regs_s", 0, 2048)])
    load("Y", "ld5", T.regs_s[:, 2048:4096], T.regs[:, 2048:4096], [("regs_s", 2048, 4096)])
    load("Y", "ld6", T.pay_s[:], T.pay[:], [("pay_s", 0, 2048)])

    kf = a("kf")
    def col(j):
        return a("cols", j, j + 1)
    home_te = [4 * t + e for t in range(RO) for e in (0, 1)]
    far_te = [4 * t + e for t in range(RO) for e in (2, 3)]
    marks = {}

    def mark(k):
        return lambda: k in marks

    def constants():
        yield iota(a("li"), [[1, 256]], 0, 0)
        yield iota(a("pi"), [[0, 2]], 0, 1)
        yield iota(a("Bm"), [[1, 8], [0, 16]], 0, 0)
        yield iota(a("rp"), [[0, 16], [1, 16]], 0, 0)
        yield iota(a("Dm"), [[1, 128]], 0, -1)
        yield fill(a("ONE"), 1.0)
        yield cp(a("crep"), a("li"))
        yield cp(a("nU1"), a("n0_i"))
        yield ts(a("pk", 0, 1), a("pi", 0, 1), 15, OP.bitwise_and)
        yield ts(a("pk", 1, 2), a("pi", 1, 2), 4, OP.arith_shift_right)
        yield cp(a("kf"), a("pk", 0, 1))
        yield cp(a("pg"), a("pk", 1, 2))
        yield fill(col(3), BETA)
        yield fill(col(14), 1.0)
        yield fill(col(15), -1.0)
        yield ts(a("BO"), a("Bm"), a("pg"), OP.is_equal)
        yield fill(a("Z"), 0.0)
        yield cp(a("Z", 15, 143, 16), a("BO", 0, 128, 16))
        for u in range(4):
            yield act(a("xr1", 1024 * u, 1024 * u + 1024), via(a("rch_s", 64 * u, 64 * u + 64), a("crep", 0, 64)), ACT.Copy)
        yield ts(a("BO16"), a("BO"), 1.0, OP.mult)
        yield ts(a("BO5"), a("BO"), 5.0, OP.mult)
        yield ts(a("rd"), a("rp"), kf, OP.subtract)
        yield ts(a("MX"), a("rd"), 0.0, OP.is_equal)
        yield ts(a("TRI"), a("Dm"), 0, OP.is_ge, 64.0, OP.mult)
        yield tt(a("TRI"), a("TRI"), a("BO"), OP.mult)
        yield fill(a("TRI", 15, 128, 16), 0.0)
        yield ts(col(0), kf, 15.0, OP.is_lt)
        yield fill(a("SIX"), 0.0625)
        yield mark("o")
        yield tt(a("E1"), a("E1"), a("E3"), OP.add)
        yield ts(a("E2"), a("ID"), col(0), OP.mult)
        yield tt(a("OHM"), a("E1"), a("E2"), OP.subtract)
        yield ts(col(1), kf, -EPS, OP.mult)
        yield ts(col(2), kf, 15.0, OP.is_equal, 16 * EPS, OP.mult)
        yield tt(col(1), col(1), col(2), OP.add)
        yield cp(a("drb", rows=96), a("dr_i", rows=96))
        yield ts(a("w_i", rows=96), a("dr_i", rows=96), 15, OP.bitwise_and)
        yield cp(a("wb", rows=96), a("w_i", rows=96))
        yield ts(a("y1"), a("rch_s"), -1.0, OP.add)
        yield ts(a("pre1"), a("n0_i"), 13.0, OP.mult, 1.0 + 10240.0, OP.add)
        for x in draws(0):
            yield x
        yield tt(a("DST", 0, 116), a("OHM", 0, 116), a("OHM", 4, 120), OP.add)
        yield tt(a("E1", 0, 116), a("OHM", 8, 124), a("OHM", 12, 128), OP.add)
        yield ts(a("E2"), a("rp", 0, 128), 4, OP.is_lt)
        yield tt(a("DST", 0, 116), a("DST", 0, 116), a("E1", 0, 116), OP.add)
        yield tt(a("DST", 0, 116), a("DST", 0, 116), a("E2", 0, 116), OP.mult)
        yield ts(col(4), kf, 320.0, OP.mult, -1.0, OP.add)
        yield ts(col(5), kf, 320.0, OP.mult, 64.0, OP.add)
        yield ts(col(6), kf, 4096.0, OP.add)
        yield mark("z")
        for x in aux_static(0):
            yield x
        marks["c"] = 1
        yield ts(col(7), kf, 2.0, OP.is_equal)
        yield ts(col(8), kf, 3.0, OP.is_equal)
        yield tt(col(7), col(7), col(8), OP.add)
        yield ts(a("BOn"), a("BO"), col(7), OP.mult)
        for j, (row, w) in enumerate(((0, 1.0), (1, 1.0), (5, 1.0), (6, 1.0), (4, -8192.0))):
            yield ts(col(9 + j), kf, float(row), OP.is_equal, w, OP.mult)
            yield ts(a("SR", 128 * j, 128 * j + 128), a("BO"), col(9 + j), OP.mult)
        yield ts(a("ZM"), a("ID"), 16.0, OP.mult)
        yield tt(a("ZM"), a("ZM"), a("BO"), OP.subtract)
        yield ts(a("ta"), a("rd"), 0.0, OP.is_gt, 16384.0, OP.mult)
        yield ts(a("tb"), a("rd"), 0.0, OP.is_equal, -8192.0, OP.mult)
        yield tt(a("ta"), a("ta"), a("tb"), OP.add)
        yield ts(a("CMh"), a("ta"), 2048.0, OP.add)
        yield ts(a("CMf"), a("ta"), 10240.0, OP.add)
        yield ts(a("RST"), a("rp"), 0, OP.is_gt)
        yield ts(a("crep1"), a("li", 0, 16), 1.0, OP.add)
        yield ts(col(8), kf, 4112.0, OP.add)
        yield fill(a("KH"), 2048.0)
        yield fill(a("KF"), 10240.0)
        yield act(a("paym"), a("pay_s"), ACT.Identity, bias=col(15))
        marks["e"] = 1

    def patterns():
        for j in (0, 1):
            yield sel(a("SEL", 128 * j, 128 * j + 128, rows=96), a("ONE", 0, 128, rows=96), [[-12, 8], [0, 16]], -home_te[j], 1)
        yield sel(a("ID"), a("ONE", 0, 128), [[-1, 128]], 0, 1)
        yield sel(a("E1"), a("BO"), [[1, 128]], -1, -1)
        yield sel(a("E3"), a("BO"), [[1, 128]], 15, -1)
        yield zeros(a("DST"))
        marks["o"] = 1
        yield zeros(a("ZT"))
        for j in range(6):
            yield sel(a("ZT", 144 * j + 15, 144 * j + 143, 16, rows=96), a("ONE", 0, 8, rows=96), [[-12, 8]], -far_te[j], 1)
        marks["z"] = 1
        yield zeros(a("send"))
        for t in range(RO):
            yield zeros(a("zr%d" % t))
        for j in range(2, 6):
            yield sel(a("SEL", 128 * j, 128 * j + 128, rows=96), a("ONE", 0, 128, rows=96), [[-12, 8], [0, 16]], -home_te[j], 1)

    def draws(t):
        for src, b in (("drb", "b6"), ("wb", "b7")):
            for j in (0, 1):
                s = 128 * (2 * t + j)
                yield mm(a(b, 256 * j, 256 * j + 256), a("SEL", s, s + 128, rows=96), a(src, rows=96))
            if src == "drb":
                yield act(a("vb%d" % t), a(b), ACT.Identity, bias=col(3))
            else:
                yield act(a("wt%d" % t), a(b), ACT.Relu, bias=col(1), scale=EPS)
        marks["v%d" % t] = 1

    def aux_static(t):
        grp = []
        for k, (src, j, row) in enumerate((("drb", 0, 0), ("drb", 1, 1), ("wb", 0, 5), ("wb", 1, 6))):
            s = 144 * (2 * t + j) + 15 - row
            grp.append(mm(a("b7", 0, 256), a("ZT", s, s + 128, rows=96), a(src, rows=96), k == 0, False))
        yield grp + [mm(a("b7", 0, 256), a("Z", 11, 139), a("SIX"), False, True)]
        yield act(a("auxS%d" % t), a("b7", 0, 256), ACT.Copy)
        marks["x%d" % t] = 1

    def relu_records():
        yield ts(a("P", 0, 2736), a("regs_s", 0, 2736), 0.0, OP.max)
        yield act(a("P", 2736, 4096), a("regs_s", 2736, 4096), ACT.Relu)
        marks["P"] = 1

    def acts_at(e, lo, hi):
        return cp(a("A%d" % e, lo, hi), via(a("acts_i"), a("nU%d" % e, lo // 16, hi // 16)))

    def acts_half(e, lo, hi):
        return ts(a("Ah%d" % e, lo, hi), a("A%d" % e, lo, hi), -2048.0, OP.add)

    YN = {1: "y1", 2: "y2", 3: "yF3", 4: "yF4"}
    YO = {1: "y2", 2: "y3", 3: "yF4", 4: "yF5"}

    def spread(e, lo, hi):
        for l in range(lo, hi, CS):
            n = min(CS, hi - l)
            yield act(a("xr", 16 * l, 16 * l + 16 * n), via(a(YN[e], l, l + n), a("crep", 0, n)), ACT.Identity, bias=col(14))

    def diag(b1, c1, src, ones, mk, b2, c2, last, n, lo, hi):
        yield mm(a(b1, c1, c1 + 128, rows=n), a(src, lo, hi), a(ones))
        yield tt(a(mk, rows=n), a(b1, c1, c1 + 128, rows=n), a("MX", 0, 128, rows=n), OP.mult)
        yield mm(a(b2, c2, c2 + n // 16), a(mk, rows=n), a(last, 0, n, 16, rows=n))

    def level(e, t, u, lo, hi):
        n = hi - lo
        bank = "b%d" % u
        tl, th = lo // 16, hi // 16
        x = "xr1" if e == 1 else "xr"
        vb, wt = ("vb%d" % t, "wt%d" % t) if e < 3 else ("vbF", "wtF")
        at = 256 * ((e - 1) % 2)
        for l in range(lo, hi, CW):
            m = min(CW, hi - l)
            for j in range(l, l + m, CG):
                c = min(CG, l + m - j)
                yield tt(a("W", 16 * j, 16 * j + 16 * c), via(a("P"), a("A%d" % e, j, j + c)), a(x, 16 * j, 16 * j + 16 * c), OP.min)
            if e == 1:
                yield mark("v%d" % t)
            for k in range(16):
                yield mm(a(bank, l - lo, l - lo + m), a("Z", 15 - k, 143 - k), a("W", 16 * l + k, 16 * l + 16 * m, 16), k == 0, k == 15)
        yield act(a("ms", lo, hi), a(bank, 0, n), ACT.Copy)
        yield mm(a(bank, n, 2 * n), a("ID"), a(wt, at + lo, at + hi), True, False)
        yield mm(a(bank, n, 2 * n), a("BO"), a("ms", lo, hi), False, True)
        yield mm(a(bank, 2 * n, 3 * n), a("TRI"), a("ms", lo, hi))
        yield tt(a("t1", lo, hi), a(bank, n, 2 * n), a(vb, at + lo, at + hi), OP.mult)
        yield tt(a("ind", lo, hi), a(bank, 2 * n, 3 * n), a("t1", lo, hi), OP.is_lt)
        yield mm(a(bank, 3 * n, 4 * n), a("OHM"), a("ind", lo, hi))

        def slots():
            yield mm(a("b4", lo, hi), a("DST"), a("ind", lo, hi))
            yield lambda: lo == 0 or "s%d_%d" % (t, lo) in marks
            yield scan(a("cum", lo, hi), a("ONE", lo, hi), a("b4", lo, hi), col(4) if lo == 0 else a("cum", lo - 1, lo))
            marks["s%d_%d" % (t, hi)] = 1
            yield tt(a("Q", lo, hi), a("b4", lo, hi), a("cum", lo, hi), OP.mult)
            for o in diag("b5", 128 * u, "Q", "BO16", "mq%d" % u, "b4", 256 + tl, "BO16", n, lo, hi):
                yield o
            yield cp(a("slot", tl, th), a("b4", 256 + tl, 256 + th))
            marks["S%d_%d" % (t, u)] = 1
        if e == 2:
            yield mark("c")
            spawn(u + 0.2, slots())
        if e in (2, 4):
            yield mark("R%d_%d_%d" % (t, e, u))
        yield tt(a("q%d" % e, lo, hi), a(bank, 3 * n, 4 * n), a("Ah%d" % e, lo, hi), OP.mult)
        for o in diag(bank, 0, "q%d" % e, "BO16", "mk%d" % u, bank, n, "BO5", n, lo, hi):
            yield o
        p = a(bank, n, n + n // 16)
        yield ts(a("rec%d" % e, tl, th), p, 0.2, OP.mult, 2048.25, OP.add)

        def reaches():
            yield tt(a(YO[e], lo, hi), via(a("P"), a("rec%d" % e, tl, th)), a(YN[e], lo, hi), OP.min)
            if e in (1, 3):
                for o in spread(e + 1, lo, hi):
                    yield o
            marks["Y%d_%d_%d" % (t, e, u)] = 1
        spawn(u - 0.5, reaches())
        yield tt(a("s_i", tl, th), p, a("pre%d" % e, tl, th), OP.add)
        yield ts(a("n_i", tl, th), a("s_i", tl, th), 2047, OP.bitwise_and)
        if e != 2:
            yield cp(a("nU%d" % (e + 1), tl, th), a("n_i", tl, th))
        if e in (1, 3):
            yield acts_at(e + 1, lo, hi)

            def rest():
                yield ts(a("pre%d" % (e + 1), tl, th), a("n_i", tl, th), 13.0, OP.mult, e + 1.0 + 10240.0, OP.add)
                yield acts_half(e + 1, lo, hi)
                marks["R%d_%d_%d" % (t, e + 1, u)] = 1
            spawn(u + 5, rest())
        yield mark("Y%d_%d_%d" % (t, e, u))

    def home(t, u, lo, hi):
        tl, th = lo // 16, hi // 16
        if t == 0:
            yield acts_at(1, lo, hi)
            yield acts_half(1, lo, hi)
        yield mark("P")
        for e in (1, 2):
            for o in level(e, t, u, lo, hi):
                yield o
        n = hi - lo
        w = n // 16
        f0, x0 = 16 * u, 256 * u
        yield cp(a("nlf", f0, f0 + w), a("n_i", tl, th))
        yield tt(a("nlf", f0 + w, f0 + 2 * w), a("n_i", tl, th), a("nlf", f0, f0 + w), OP.subtract)
        yield tt(a("nx", x0, x0 + 2 * n), via(a("nlf", f0, f0 + 2 * w), a("crep", 0, 2 * w)), a("MX", 0, 2 * n), OP.mult)
        yield mark("x%d" % t)
        yield [mm(a("b6", lo, hi), a("ID"), a("auxS%d" % t, lo, hi), True, False),
               mm(a("b6", lo, hi), a("Z", 13, 141), a("nx", x0, x0 + n), False, False),
               mm(a("b6", lo, hi), a("Z", 12, 140), a("nx", x0 + n, x0 + 2 * n), False, True)]
        yield act(a("auxB", lo, hi), a("b6", lo, hi), ACT.Copy)
        yield mark("S%d_%d" % (t, u))
        yield scatter(a("send", 0, 1216), a("slot", tl, th), a("y3", lo, hi))
        marks["y%d_%d" % (t, lo)] = 1
        yield lambda: all("y%d_%d" % (t, l) in marks for l, h in HUN)
        yield scatter(a("send", 64, 1280), a("slot", tl, th), a("auxB", lo, hi))

    def depart(t):
        order("G", [("zr%d" % t, 0, 1280)], [])
        for r in others:
            do(send(r, a("send", REG * r, REG * r + 128), T["land%d" % t][:, 128 * me:128 * me + 128], "a%d_%d" % (t, me), "la%d_%d" % (t, r)))
        for i, r in enumerate(others):
            arrives("a%d_%d" % (t, r), [("land%d" % t, 128 * r, 128 * r + 128)], free["G"] + 2700.0 + 500.0 * i)
            arrives("z%d_%d" % (t, r), [("zr%d" % t, REG * r, REG * r + 64)], free["G"] + 30000.0)

    def far(t, u, ps, lo, hi):
        tl, th = lo // 16, hi // 16
        n = hi - lo
        bank = "b%d" % u
        for p in ps:
            name, s = ("send", REG * me) if p == 0 else ("land%d" % t, 128 * place[p])
            yield act(a("auxF", 64 * p, 64 * p + 64), a(name, s + 64, s + 128), ACT.Copy)
            yield act(a("yF3", 64 * p, 64 * p + 64), a(name, s, s + 64), ACT.Copy)
        for o in spread(3, lo, hi):
            yield o
        for o in diag("b5", 128 * u, "auxF", "BOn", "mq%d" % u, "b4", tl, "BO16", n, lo, hi):
            yield o
        for j in (0, 2, 1, 3):
            yield mm(a(bank, n * j, n * j + n), a("SR", 128 * j, 128 * j + 128), a("auxF", lo, hi))
        yield cp(a("nU3", tl, th), a("b4", tl, th))
        yield acts_at(3, lo, hi)
        for j in (0, 1):
            yield act(a("vbF", 256 * j + lo, 256 * j + hi), a(bank, n * j, n * j + n), ACT.Identity, bias=col(3))
            yield act(a("wtF", 256 * j + lo, 256 * j + hi), a(bank, n * (2 + j), n * (3 + j)), ACT.Relu, bias=col(1), scale=EPS)
        yield ts(a("pre3", tl, th), a("b4", tl, th), 13.0, OP.mult, 3.0 + 10240.0, OP.add)
        yield acts_half(3, lo, hi)
        for e in (3, 4):
            for o in level(e, t, u, lo, hi):
                yield o
        marks["g%d_%d" % (t, u)] = 1
        yield tt(a("lv", lo, hi), via(a("paym"), a("nU5", tl, th)), a("yF5", lo, hi), OP.min)
        yield mm(a(bank, 0, n), a("ZM"), a("lv", lo, hi))
        yield act(a("zF", lo, hi), a(bank, 0, n), ACT.Sign)
        for p in ps:
            r = place[p]
            if p:
                yield send(r, a("zF", 64 * p, 64 * p + 64), T["zr%d" % t][:, REG * me:REG * me + 64], "z%d_%d" % (t, me), "lz%d_%d" % (t, r))
            else:
                yield act(a("zr%d" % t, REG * me, REG * me + 64), a("zF", 0, 64), ACT.Copy)
        yield tt(a("NV", lo, hi), via(a("regs_s", 0, 4096), a("rec4", tl, th)), a("zF", lo, hi), OP.add)
        yield ts(a("NV", lo, hi), a("NV", lo, hi), 15.0, OP.min, -15.0, OP.max)
        marks["f%d_%d" % (t, u)] = 1

    def first_of(n, q, cm, kc, extra, rec):
        b = "b7" if n == "h" else "b6"
        yield ts(a("rf8" + n), a(rec), 2.0 ** -13, OP.mult)
        yield [mm(a(b, 0, 256), a("BO16"), a(q), True, False), mm(a(b, 0, 256), a("ID"), a(cm), False, False),
               mm(a(b, 0, 256), extra[0], extra[1], False, True)]
        yield [mm(a(b, 256, 512), a("BO16"), a(q), True, False), mm(a(b, 256, 512), a("ID"), a(kc), False, False),
               mm(a(b, 256, 512), extra[0], extra[1], False, True)]
        yield act(a("Y" + n), via(a("rf8" + n), a("crep", 0, 16)), ACT.Copy, scale=8192.0)
        yield act(a("Z2" + n, 0, 240), via(a("rf8" + n), a("crep1", 0, 15)), ACT.Copy, scale=8192.0)
        yield tt(a("eq" + n), a(b, 0, 256), a("Y" + n), OP.is_equal)
        yield scan(a("lc" + n), a("RST"), a("eq" + n), 0.0)
        yield tt(a("er" + n, 0, 240), a(b, 256, 496), a("Z2" + n, 0, 240), OP.is_equal)
        yield tt(a("u" + n), a("lc" + n, 15, 256, 16), a("rf8" + n), OP.add)
        yield scan(a("ld" + n, 0, 240), a("RST", 0, 240), a("er" + n, 0, 240), 0.0)
        yield ts(a("off" + n, 0, 16, 2), a("u" + n, 0, 16, 2), 8192.0, OP.mult, col(6), OP.min)
        yield tt(a("u" + n, 1, 16, 2), a("u" + n, 1, 16, 2), a("ld" + n, 15, 240, 32), OP.add)
        yield ts(a("off" + n, 1, 16, 2), a("u" + n, 1, 16, 2), 8192.0, OP.mult, col(8), OP.min)

    def change(n, blocks, values):
        for c in blocks:
            yield scatter(a("regs_s"), a("off" + n, 2 * c, 2 * c + 2), a(values, 32 * c, 32 * c + 32))

    def waiting(t):
        yield mark("e")
        yield ts(a("ng"), a("Q"), col(5), OP.is_ge, 8192.0, OP.mult)
        for o in first_of("h", "q2", "CMh", "KH", (a("BO"), a("ng")), "rec2"):
            yield o
        if t + 1 < RO:
            yield zeros(a("send"))
            for o in draws(t + 1):
                yield o
            for o in aux_static(t + 1):
                yield o

    def leaves(t):
        yield lambda: all("g%d_%d" % (t, u) in marks for u in range(len(FUN)))
        for o in first_of("f", "q4", "CMf", "KF", (a("SR", 512, 640), a("auxF")), "rec4"):
            yield o
        yield lambda: all("f%d_%d" % (t, u) in marks for u in range(len(FUN)))
        for o in change("f", [2 * place.index(r) + c for r in (3, 2, 1, 0) for c in (1, 0)], "NV"):
            yield o
        for lo in (128, 0):
            yield act(a("zl", lo, lo + 128), via(a("zr%d" % t), a("slot", lo // 16, lo // 16 + 8)), ACT.Copy, scale=-1.0)
        for lo in (128, 0):
            yield tt(a("HV", lo, lo + 128), via(a("regs_s", 0, 4096), a("rec2", lo // 16, lo // 16 + 8)), a("zl", lo, lo + 128), OP.add)
        for lo in (128, 0):
            yield ts(a("HV", lo, lo + 128), a("HV", lo, lo + 128), 15.0, OP.min, -15.0, OP.max)
        for o in change("h", list(range(7, -1, -1)), "HV"):
            yield o

    for t in range(RO):
        jobs = [(u, home(t, u, lo, hi)) for u, (lo, hi) in enumerate(HUN)]
        if t == 0:
            c = constants()
            for i in range(17):
                do(next(c))
            together([(9, c), (8, relu_records()), (9, patterns())] + jobs)
        else:
            for o in relu_records():
                do(o)
            together(jobs)
        depart(t)
        together([(u, far(t, u, FU[u], lo, hi)) for u, (lo, hi) in enumerate(FUN)] + [(8, waiting(t)), (7, leaves(t))])

    order("Y", [("regs_s", 0, 4128)], [])
    g.sync.dma_start(T.yr[:], T.regs_s[:, 0:4096]).then_inc(T.sem.yo, 16)
    g.sync.wait_ge(T.sem.yo, 16)
    for s in ("eV", "eP", "eS", "eG"):
        g.sync.wait_ge(T.sem[s], count[s])
    for i in range(7):
        g.sync.wait_ge(T.sem["ld%d" % i], 16)
    for t in range(RO):
        for r in others:
            for k in ("a", "z", "la", "lz"):
                g.sync.wait_ge(T.sem["%s%d_%d" % (k, t, r)], 8)
